import numpy as np
import ml_dtypes


def mxq(x, axis, fmt="e4m3"):
    dtype, down = {"e4m3": (ml_dtypes.float8_e4m3fn, 7), "e5m2": (ml_dtypes.float8_e5m2, 14)}[fmt]
    v = np.moveaxis(np.asarray(x, np.float32).astype(ml_dtypes.bfloat16).astype(np.float64), axis, -1)
    blocks = v.reshape(v.shape[:-1] + (-1, 32))
    amax = np.abs(blocks).max(-1, keepdims=True)
    byte = np.maximum(np.where(amax > 0, np.frexp(amax)[1] - 1 + 127, 0) - down, 1)
    scale = np.exp2(byte - 127.0)
    codes = (blocks / scale).astype(np.float32).astype(dtype).astype(np.float64)
    return np.moveaxis((codes * scale).reshape(v.shape), -1, axis)


WIDE = False


def mx_kscale(k):
    if not WIDE:
        return np.ones(k)
    levels = np.array([10, -10, 5, -5, 0])
    if k % 512:
        return np.exp2(np.random.permutation(np.resize(levels, k // 32))).repeat(32)
    a = np.empty((k // 512, 16))
    for p in range(k // 512):
        a[p, :8] = np.random.permutation(np.resize(levels, 8))
        for g in range(8):
            far = levels[np.abs(levels - a[p, g]) >= 10]
            a[p, g + 8] = far[np.random.randint(len(far))]
    return np.exp2(a.ravel()).repeat(32)


def f64(x):
    return np.asarray(x).astype(np.float64)


def striped(idx):
    return np.tile(idx.reshape(-1, 16).T, (8, 1)).astype(np.uint16)


def unstriped(offs):
    return offs[:16].T.reshape(-1).astype(np.int64)


E2M1 = np.array([0.0, 0.5, 1.0, 1.5, 2.0, 3.0, 4.0, 6.0, -0.0, -0.5, -1.0, -1.5, -2.0, -3.0, -4.0, -6.0])


def pack_weight(w, fmt):
    k, n = w.shape
    w = f64(np.asarray(w, np.float32).astype(ml_dtypes.bfloat16)).reshape(k // 32, 32, n)
    amax = np.abs(w).max(1)
    if fmt == "e4m3":
        byte = np.frexp(amax)[1] - 1 + 127 - 7
    else:
        mant, ex = np.frexp(amax / 6.0)
        byte = np.where(mant > 0.5, ex, ex - 1) + 127
    byte = np.clip(np.where(amax > 0, byte, 1), 1, 254)
    scaled = (w * np.exp2(127.0 - byte)[:, None, :]).reshape(k, n).astype(np.float32)
    by_word = np.ascontiguousarray(scaled.reshape(k // 512, 128, 4, n).transpose(0, 1, 3, 2))
    if fmt == "e4m3":
        words = by_word.astype(ml_dtypes.float8_e4m3fn).view(np.uint8)
    else:
        c = by_word.astype(ml_dtypes.float4_e2m1fn).view(np.uint8) & 0xF
        words = (c[..., 0::2] | (c[..., 1::2] << 4)).reshape(k // 512, 128, 2 * n)
    return np.ascontiguousarray(words), np.ascontiguousarray(byte.astype(np.uint8).reshape(k // 512, 16, n))


def unpack_weight(words, scales, fmt):
    g, _, n = scales.shape
    words = np.ascontiguousarray(words).reshape(g, 128, n, -1)
    if fmt == "e4m3":
        vals = words.view(ml_dtypes.float8_e4m3fn).astype(np.float64)
    else:
        nib = np.empty((g, 128, n, 4), np.uint8)
        nib[..., 0::2] = words & 0xF
        nib[..., 1::2] = words >> 4
        vals = E2M1[nib]
    vals = vals * np.repeat(np.exp2(scales.astype(np.float64) - 127.0), 8, axis=1)[..., None]
    return vals.transpose(0, 1, 3, 2).reshape(g * 512, n)


def gelu(v):
    return 0.5 * v * (1.0 + np.tanh(np.sqrt(2.0 / np.pi) * (v + 0.044715 * v**3)))


def bf(x):
    return np.asarray(x, np.float32).astype(ml_dtypes.bfloat16)


def planes(Y):
    n, m = Y.shape
    b = f64(bf(Y)).reshape(n // 32, 32, m)
    amax = np.abs(b).max(1)
    byte = np.clip(np.where(amax > 0, np.frexp(amax)[1] - 1 + 127 - 7, 1), 1, 254)
    codes = (b * np.exp2(127.0 - byte)[:, None, :]).reshape(n, m).astype(np.float32).astype(ml_dtypes.float8_e4m3fn).view(np.uint8)
    words = codes.reshape(n // 512, 128, 4, m).transpose(0, 1, 3, 2)
    return np.ascontiguousarray(words), np.ascontiguousarray(byte.astype(np.uint8).reshape(n // 512, 16, m))


K, H, N, T, S = 1024, 512, 384, 4096, 1024


def setup_inputs():
    n = np.random.standard_normal
    s = mx_kscale(K)[:, None]
    u = mx_kscale(H)[:, None]
    tab_words, tab_scales = pack_weight(n((K, T)) * s, "e4m3")
    offs = striped(np.random.permutation(T)[:S])
    w1 = (n((K, H)) / np.sqrt(K) / s * u.T).astype(np.float32)
    w2_words, w2_scales = pack_weight(n((K, H)) / np.sqrt(K) / s * u.T, "e2m1")
    w3_words, w3_scales = pack_weight(n((K, H)) / np.sqrt(K) / s * u.T, "e4m3")
    w4 = (n((H, N)) / np.sqrt(H) / u).astype(np.float32)
    w5_words, w5_scales = pack_weight(n((K, N)) / np.sqrt(K) / s, "e2m1")
    prior = n((N, S)).astype(np.float32)
    return {"tab_words": tab_words, "tab_scales": tab_scales, "offs": offs,
            "w1": w1, "w2_words": w2_words, "w2_scales": w2_scales,
            "w3_words": w3_words, "w3_scales": w3_scales, "w4": w4,
            "w5_words": w5_words, "w5_scales": w5_scales, "prior": prior}


def reference(tab_words, tab_scales, offs, w1, w2_words, w2_scales,
              w3_words, w3_scales, w4, w5_words, w5_scales, prior):
    v = unpack_weight(tab_words, tab_scales, "e4m3")[:, unstriped(offs)]
    a = mxq(f64(w1), 0, "e4m3").T @ v
    b = unpack_weight(w2_words, w2_scales, "e2m1").T @ v
    c = unpack_weight(w3_words, w3_scales, "e4m3").T @ v
    h = np.abs(a - b) + c
    words, scales = planes(h)
    e = mxq(f64(w4), 0, "e4m3").T @ mxq(h, 0, "e4m3")
    d = unpack_weight(w5_words, w5_scales, "e2m1").T @ v
    y = e / (1.0 + np.exp(-e)) + d + f64(prior)
    return y, h, words, scales

@@ -1,0 +1,259 @@
+from contextlib import ExitStack
+
+import concourse.mybir as mybir
+
+K, H, N, T, S = 1024, 512, 384, 4096, 1024
+FLOPS = 2 * S * (3 * K * H + H * N + K * N)
+
+F32 = mybir.dt.float32
+BF16 = mybir.dt.bfloat16
+I32 = mybir.dt.int32
+U32 = mybir.dt.uint32
+U16 = mybir.dt.uint16
+U8 = mybir.dt.uint8
+FP8X4 = mybir.dt.float8_e4m3fn_x4
+FP4X4 = mybir.dt.float4_e2m1fn_x4
+ACT = mybir.ActivationFunctionType
+ALU = mybir.AluOpType
+
+P = 128
+PACK = 4
+PASSES = 2
+HALF = 512
+HALVES = 2
+NBLK = N // P
+QUADS = 4
+W1_SCALAR_M = 48
+ROW0 = 96
+SC_W2, SC_W3, SC_W5, SC_COLS = S, S + H, S + 2 * H, S + 2 * H + N
+H_SCALAR_COLS = (512, 192)
+
+
+def tile_list_invoice_fraud_screen_kernel(tc, tab_words, tab_scales, offs, w1, w2_words, w2_scales,
+                                                   w3_words, w3_scales, w4, w5_words, w5_scales, prior,
+                                                   out_0, out_1, out_2, out_3):
+    nc = tc.nc
+    with ExitStack() as ctx:
+        keep = ctx.enter_context(tc.tile_pool(name="keep", bufs=1))
+        ring = ctx.enter_context(tc.tile_pool(name="ring", bufs=3))
+        reuse = ctx.enter_context(tc.tile_pool(name="reuse", bufs=1))
+        psum = ctx.enter_context(tc.psum_pool(name="psum", bufs=1))
+
+        def held(shape, dtype, name):
+            return keep.tile(shape, dtype, name=name, align_bytes=64)
+
+        taken = []
+
+        def bank():
+            taken.append(len(taken) % 8)
+            return psum.tile([P, HALF], F32, name="bank%d" % taken[-1])
+
+        def again(shape, dtype, name, offset):
+            return reuse.tile(shape, dtype, name=name, align_bytes=64, offset=offset)
+
+        offsets = keep.tile([P, S // 16], U16, name="offsets")
+        tab_sc = held([P, T], U8, "tab_sc")
+        w23_sc_raw = again([P, 2, H], U8, "w23_sc_raw", 4 * T)
+        rows = held([P, SC_COLS], U8, "rows")
+        planes = held([P, PASSES, SC_COLS], U8, "planes")
+        warm_in = held([P, 8], F32, "warm_in")
+        warm_out = held([P, 8], F32, "warm_out")
+
+        nc.vector.memset(tab_sc[:ROW0].bitcast(I32), 0)
+        nc.vector.memset(w23_sc_raw[:ROW0].bitcast(I32), 0)
+        nc.gpsimd.memset(warm_in[:], 0.0)
+        nc.gpsimd.memset(planes[:].bitcast(I32), 0)
+        nc.scalar.activation(warm_out[:], warm_in[:], ACT.Silu)
+
+        def load_rows(dst, src):
+            nc.sync.dma_start(dst.bitcast(I32), src.rearrange("a q n -> q a n").bitcast(I32))
+
+        nc.sync.dma_start(offsets[:], offs)
+        load_rows(tab_sc[ROW0:, :], tab_scales)
+        load_rows(w23_sc_raw[ROW0:, 0, :], w2_scales)
+        load_rows(w23_sc_raw[ROW0:, 1, :], w3_scales)
+        load_rows(rows[ROW0:, SC_W5:], w5_scales)
+        w3_raw = held([P, PASSES, H], I32, "w3_raw")
+        nc.sync.dma_start(w3_raw[:], w3_words.rearrange("a p c i -> p a (c i)").bitcast(I32))
+        tab = [again([P, T], I32, "tab%d" % a, 4 * T * a) for a in range(PASSES)]
+        nc.sync.dma_start(tab[0][:], tab_words[0].rearrange("p t i -> p (t i)").bitcast(I32))
+        w2_raw = held([P, PASSES, 2 * H], U8, "w2_raw")
+        nc.sync.dma_start(w2_raw[:].bitcast(I32), w2_words.rearrange("a p c -> p a c").bitcast(I32))
+        w1_raw = [again([P, PACK, H], F32, "w1_raw%d" % a, 8192 * a) for a in range(PASSES)]
+
+        def load_w1(a):
+            nc.sync.dma_start(w1_raw[a][:], w1[512 * a:512 * (a + 1), :].rearrange("(p j) c -> p j c", j=PACK))
+
+        v_sc = again([P, S], U8, "v_sc", 4 * T + 1024)
+        nc.vector.tensor_copy(v_sc[:], tab_sc[:].indirect(offsets[:]))
+        nc.vector.tensor_copy(rows[:, SC_W2:SC_W5].rearrange("p (w t m) -> p w m t", w=2, t=PACK),
+                              w23_sc_raw[:].rearrange("p w (m t) -> p w m t", t=PACK))
+        nc.vector.tensor_copy(rows[:, :S].bitcast(I32), v_sc[:].bitcast(I32))
+        for q in range(QUADS):
+            nc.sync.dma_start(planes[32 * q:32 * q + 4].bitcast(I32), rows[ROW0 + 8 * q:ROW0 + 8 * q + 8, :].bitcast(I32))
+        nc.sync.dma_start(tab[1][:], tab_words[1].rearrange("p t i -> p (t i)").bitcast(I32))
+
+        w3 = held([P, PASSES, H], I32, "w3")
+        nc.vector.tensor_copy(w3[:].rearrange("p a (t m) -> p a m t", t=PACK), w3_raw[:].rearrange("p a (m t) -> p a m t", t=PACK))
+
+        v = {}
+
+        def gather(a, s):
+            v[a, s] = held([P, HALF], U32, "v%d%d" % (a, s))
+            nc.vector.tensor_copy(v[a, s][:], tab[a][:].bitcast(U32).indirect(offsets[:, 32 * s:32 * (s + 1)]))
+
+        gather(0, 0)
+        w2 = held([P, PASSES, 2 * H], U8, "w2")
+        nc.vector.tensor_copy(w2[:].rearrange("p a (t m b) -> p a m t b", t=PACK, b=2),
+                              w2_raw[:].rearrange("p a (m t b) -> p a m t b", t=PACK, b=2))
+        gather(0, 1)
+        load_w1(0)
+        load_w1(1)
+
+        def moving(a, s):
+            return v[a, s][:].bitcast(FP8X4), planes[:, a, HALF * s:HALF * (s + 1)]
+
+        def plane(a, first, block):
+            return planes[:, a, first + P * block:first + P * (block + 1)]
+
+        def mm(acc, lhsT, lhsT_scale, rhs, start, stop):
+            nc.tensor.matmul_mx(out=acc[:], lhsT=lhsT, lhsT_scale=lhsT_scale, rhs=rhs[0], rhs_scale=rhs[1], start=start, stop=stop)
+
+        w1q = [held([P, H], U32, "w1q%d" % a) for a in range(PASSES)]
+        w1_sc = [held([P, H], U8, "w1_sc%d" % a) for a in range(PASSES)]
+
+        def mm_c(acc, a, s, t):
+            cols = slice(P * t, P * (t + 1))
+            mm(acc, w3[:, a, cols].bitcast(FP8X4), plane(a, SC_W3, t), moving(a, s), a == 0, a == 1)
+
+        def mm_b(acc, a, s, t):
+            mm(acc, w2[:, a, 2 * P * t:2 * P * (t + 1)].bitcast(FP4X4), plane(a, SC_W2, t), moving(a, s), a == 0, False)
+
+        def mm_a(acc, a, s, t):
+            cols = slice(P * t, P * (t + 1))
+            mm(acc, w1q[a][:, cols].bitcast(FP8X4), w1_sc[a][:, cols], moving(a, s), False, a == 1)
+
+        def quant_w1(a):
+            grouped = held([P, PACK, P, PACK], BF16, "w1g%d" % a)
+            dst = grouped[:].rearrange("p t m j -> p m t j")
+            src = w1_raw[a][:].rearrange("p j (m t) -> p m t j", t=PACK)
+            nc.scalar.activation(dst[:, :W1_SCALAR_M], src[:, :W1_SCALAR_M], ACT.Copy, scale=-1.0)
+            nc.vector.tensor_scalar(dst[:, W1_SCALAR_M:], src[:, W1_SCALAR_M:], -1.0, None, ALU.mult)
+            nc.vector.quantize_mx(out=w1q[a][:].bitcast(FP8X4), scales=w1_sc[a][:], in_=grouped[:].rearrange("p t m j -> p (t m j)"))
+
+        h = [held([P, PACK, HALF], F32, "h%d" % s) for s in range(HALVES)]
+        hq = held([P, S], U32, "hq")
+        h_sc = held([P, S], U8, "h_sc")
+        out1_v = out_1.rearrange("(p t) j -> p t j", t=PACK)
+        out2_v = out_2[0].rearrange("p m i -> p (m i)").bitcast(I32)
+
+        def finish_slice(s, t, diff, third):
+            mag = ring.tile([P, HALF], F32, name="mag")
+            nc.scalar.activation(mag[:], diff[:], ACT.Abs)
+            nc.vector.tensor_tensor(h[s][:, t, :], mag[:], third[:], ALU.add)
+            if t % 2 == 1:
+                nc.sync.dma_start(out1_v[:, t - 1:t + 1, HALF * s:HALF * (s + 1)], h[s][:, t - 1:t + 1, :])
+
+        def quant_h(s):
+            grouped = held([P, HALF, PACK], BF16, "hg%d" % s)
+            dst = grouped[:].rearrange("p (c i) t -> p c t i", i=4)
+            src = h[s][:].rearrange("p t (c i) -> p c t i", i=4)
+            cut = H_SCALAR_COLS[s] // 4
+            for c0 in range(0, cut, 32):
+                c1 = min(cut, c0 + 32)
+                nc.scalar.activation(dst[:, c0:c1], src[:, c0:c1], ACT.Copy)
+            if cut < HALF // 4:
+                nc.vector.tensor_copy(dst[:, cut:], src[:, cut:])
+            cols = slice(HALF * s, HALF * (s + 1))
+            nc.vector.quantize_mx(out=hq[:, cols].bitcast(FP8X4), scales=h_sc[:, cols], in_=grouped[:].rearrange("p c t -> p (c t)"))
+            nc.sync.dma_start(out2_v[:, cols], hq[:, cols].bitcast(I32))
+
+        pairs = [(bank(), bank()) for t in range(PACK)]
+        diff = [pair[0] for pair in pairs]
+        third = [pair[1] for pair in pairs]
+        for t in range(PACK):
+            mm_c(third[t], 0, 0, t)
+        for t in range(PACK):
+            mm_b(diff[t], 0, 0, t)
+        gather(1, 0)
+        for t in range(PACK):
+            mm_c(third[t], 1, 0, t)
+        for t in range(PACK):
+            mm_b(diff[t], 1, 0, t)
+        gather(1, 1)
+        w4_raw = again([P, PACK, N], F32, "w4_raw", 4 * T + 8192)
+        w5 = again([P, PASSES, 2 * N], U8, "w5", 4 * T)
+        nc.sync.dma_start(w5[:].bitcast(I32), w5_words.rearrange("a p c -> p a c").bitcast(I32))
+        nc.sync.dma_start(w4_raw[:], w4.rearrange("(p j) n -> p j n", j=PACK))
+        prior_sb = [again([P, NBLK, HALF], F32, "prior0", 4 * T + 2048), again([P, NBLK, HALF], F32, "prior1", 0)]
+
+        def load_prior(s):
+            nc.sync.dma_start(prior_sb[s][:], prior[:, HALF * s:HALF * (s + 1)].rearrange("(b p) j -> p b j", p=P))
+
+        load_prior(0)
+        quant_w1(0)
+        load_prior(1)
+        for t in range(PACK):
+            mm_a(diff[t], 0, 0, t)
+        quant_w1(1)
+        for t in range(PACK):
+            mm_a(diff[t], 1, 0, t)
+            finish_slice(0, t, diff[t], third[t])
+
+        w4g = held([P, N, PACK], BF16, "w4g")
+        w4q = held([P, N], U32, "w4q")
+        w4_sc = held([P, N], U8, "w4_sc")
+
+        def quant_w4():
+            nc.scalar.activation(w4g[:].rearrange("p (c i) j -> p c j i", i=4), w4_raw[:].rearrange("p j (c i) -> p c j i", i=4), ACT.Copy)
+            flat = w4g[:].rearrange("p n j -> p (n j)")
+            for n0, n1 in ((0, 256), (256, 384)):
+                nc.vector.quantize_mx(out=w4q[:, n0:n1].bitcast(FP8X4), scales=w4_sc[:, n0:n1], in_=flat[:, 4 * n0:4 * n1])
+
+        def second_slice(t):
+            dif = bank()
+            thi = bank()
+            for a in range(PASSES):
+                mm_b(dif, a, 1, t)
+            for a in range(PASSES):
+                mm_a(dif, a, 1, t)
+            for a in range(PASSES):
+                mm_c(thi, a, 1, t)
+            finish_slice(1, t, dif, thi)
+
+        base = {}
+
+        def direct(s):
+            for b in range(NBLK):
+                acc = bank()
+                for a in range(PASSES):
+                    mm(acc, w5[:, a, 2 * P * b:2 * P * (b + 1)].bitcast(FP4X4), plane(a, SC_W5, b),
+                       moving(a, s), a == 0, a == 1)
+                base[s, b] = held([P, HALF], F32, "base%d%d" % (s, b))
+                nc.vector.tensor_tensor(base[s, b][:], prior_sb[s][:, b, :], acc[:], ALU.add)
+
+        def scores(s):
+            cols = slice(HALF * s, HALF * (s + 1))
+            for b in range(NBLK):
+                acc = bank()
+                mm(acc, w4q[:, P * b:P * (b + 1)].bitcast(FP8X4), w4_sc[:, P * b:P * (b + 1)],
+                   (hq[:, cols].bitcast(FP8X4), h_sc[:, cols]), True, True)
+                gate = ring.tile([P, HALF], F32, name="gate")
+                nc.scalar.activation(gate[:], acc[:], ACT.Silu)
+                y = held([P, HALF], F32, "y%d%d" % (s, b))
+                nc.vector.tensor_tensor(y[:], gate[:], base[s, b][:], ALU.add)
+                nc.sync.dma_start(out_0[P * b:P * (b + 1), cols], y[:])
+
+        second_slice(0)
+        quant_w4()
+        quant_h(0)
+        direct(0)
+        second_slice(1)
+        second_slice(2)
+        scores(0)
+        second_slice(3)
+        direct(1)
+        quant_h(1)
+        for q in range(QUADS):
+            nc.sync.dma_start(out_3[0, 4 * q:4 * q + 4, :].bitcast(I32), h_sc[32 * q:32 * q + 4, :].bitcast(I32))
+        scores(1)

@@ -18,15 +18,20 @@ ALU = mybir.AluOpType
 
 P = 128
 PACK = 4
-PASSES = 2
+K_PASS = P * PACK
+PASSES = K // K_PASS
 HALF = 512
-HALVES = 2
+HALVES = S // HALF
 NBLK = N // P
 QUADS = 4
-W1_SCALAR_M = 48
+BANKS = 8
 ROW0 = 96
 SC_W2, SC_W3, SC_W5, SC_COLS = S, S + H, S + 2 * H, S + 2 * H + N
-H_SCALAR_COLS = (512, 192)
+TAB_BYTES = 4 * T
+TAB0_AT = 6144
+TAB1_AT = TAB0_AT + TAB_BYTES + 6144
+W1_SCALAR_M = 48
+W1_LAST_SCALAR_M = 24
 
 
 def tile_list_invoice_fraud_screen_kernel(tc, tab_words, tab_scales, offs, w1, w2_words, w2_scales,
@@ -35,32 +40,31 @@ def tile_list_invoice_fraud_screen_kernel(tc, tab_words, tab_scales, offs, w1, w
     nc = tc.nc
     with ExitStack() as ctx:
         keep = ctx.enter_context(tc.tile_pool(name="keep", bufs=1))
-        ring = ctx.enter_context(tc.tile_pool(name="ring", bufs=3))
         reuse = ctx.enter_context(tc.tile_pool(name="reuse", bufs=1))
         psum = ctx.enter_context(tc.psum_pool(name="psum", bufs=1))
 
         def held(shape, dtype, name):
             return keep.tile(shape, dtype, name=name, align_bytes=64)
 
+        def placed(shape, dtype, name, offset):
+            return reuse.tile(shape, dtype, name=name, align_bytes=64, offset=offset)
+
         taken = []
 
         def bank():
-            taken.append(len(taken) % 8)
+            taken.append(len(taken) % BANKS)
             return psum.tile([P, HALF], F32, name="bank%d" % taken[-1])
-
-        def again(shape, dtype, name, offset):
-            return reuse.tile(shape, dtype, name=name, align_bytes=64, offset=offset)
 
         offsets = keep.tile([P, S // 16], U16, name="offsets")
         tab_sc = held([P, T], U8, "tab_sc")
-        w23_sc_raw = again([P, 2, H], U8, "w23_sc_raw", 4 * T)
+        w23_sc_raw = held([P, 2, H], U8, "w23_sc_raw")
         rows = held([P, SC_COLS], U8, "rows")
         planes = held([P, PASSES, SC_COLS], U8, "planes")
         warm_in = held([P, 8], F32, "warm_in")
         warm_out = held([P, 8], F32, "warm_out")
 
-        nc.vector.memset(tab_sc[:ROW0].bitcast(I32), 0)
         nc.vector.memset(w23_sc_raw[:ROW0].bitcast(I32), 0)
+        nc.vector.memset(tab_sc[:ROW0].bitcast(I32), 0)
         nc.gpsimd.memset(warm_in[:], 0.0)
         nc.gpsimd.memset(planes[:].bitcast(I32), 0)
         nc.scalar.activation(warm_out[:], warm_in[:], ACT.Silu)
@@ -68,33 +72,35 @@ def tile_list_invoice_fraud_screen_kernel(tc, tab_words, tab_scales, offs, w1, w
         def load_rows(dst, src):
             nc.sync.dma_start(dst.bitcast(I32), src.rearrange("a q n -> q a n").bitcast(I32))
 
+        def load_table(a):
+            nc.sync.dma_start(tab[a][:], tab_words[a].rearrange("p t i -> p (t i)").bitcast(I32))
+
+        def load_w1(dst, a, cols):
+            nc.sync.dma_start(dst[:], w1[K_PASS * a:K_PASS * (a + 1), cols].rearrange("(p j) c -> p j c", j=PACK))
+
+        def load_prior(s):
+            nc.sync.dma_start(prior_sb[s][:], prior[:, HALF * s:HALF * (s + 1)].rearrange("(b p) j -> p b j", p=P))
+
+        tab = [placed([P, T], I32, "tab0", TAB0_AT), placed([P, T], I32, "tab1", TAB1_AT)]
+        w2_raw = held([P, PASSES, 2 * H], U8, "w2_raw")
         nc.sync.dma_start(offsets[:], offs)
-        load_rows(tab_sc[ROW0:, :], tab_scales)
         load_rows(w23_sc_raw[ROW0:, 0, :], w2_scales)
         load_rows(w23_sc_raw[ROW0:, 1, :], w3_scales)
+        load_rows(tab_sc[ROW0:, :], tab_scales)
         load_rows(rows[ROW0:, SC_W5:], w5_scales)
-        w3_raw = held([P, PASSES, H], I32, "w3_raw")
-        nc.sync.dma_start(w3_raw[:], w3_words.rearrange("a p c i -> p a (c i)").bitcast(I32))
-        tab = [again([P, T], I32, "tab%d" % a, 4 * T * a) for a in range(PASSES)]
-        nc.sync.dma_start(tab[0][:], tab_words[0].rearrange("p t i -> p (t i)").bitcast(I32))
-        w2_raw = held([P, PASSES, 2 * H], U8, "w2_raw")
+        load_table(0)
         nc.sync.dma_start(w2_raw[:].bitcast(I32), w2_words.rearrange("a p c -> p a c").bitcast(I32))
-        w1_raw = [again([P, PACK, H], F32, "w1_raw%d" % a, 8192 * a) for a in range(PASSES)]
+        w1_first = held([P, PACK, H], F32, "w1_first")
+        load_w1(w1_first, 0, slice(0, H))
 
-        def load_w1(a):
-            nc.sync.dma_start(w1_raw[a][:], w1[512 * a:512 * (a + 1), :].rearrange("(p j) c -> p j c", j=PACK))
-
-        v_sc = again([P, S], U8, "v_sc", 4 * T + 1024)
-        nc.vector.tensor_copy(v_sc[:], tab_sc[:].indirect(offsets[:]))
+        v_sc = placed([P, S], U8, "v_sc", TAB1_AT)
         nc.vector.tensor_copy(rows[:, SC_W2:SC_W5].rearrange("p (w t m) -> p w m t", w=2, t=PACK),
                               w23_sc_raw[:].rearrange("p w (m t) -> p w m t", t=PACK))
+        nc.vector.tensor_copy(v_sc[:], tab_sc[:].indirect(offsets[:]))
         nc.vector.tensor_copy(rows[:, :S].bitcast(I32), v_sc[:].bitcast(I32))
-        for q in range(QUADS):
+        for q in (0, 2, 1, 3):
             nc.sync.dma_start(planes[32 * q:32 * q + 4].bitcast(I32), rows[ROW0 + 8 * q:ROW0 + 8 * q + 8, :].bitcast(I32))
-        nc.sync.dma_start(tab[1][:], tab_words[1].rearrange("p t i -> p (t i)").bitcast(I32))
-
-        w3 = held([P, PASSES, H], I32, "w3")
-        nc.vector.tensor_copy(w3[:].rearrange("p a (t m) -> p a m t", t=PACK), w3_raw[:].rearrange("p a (m t) -> p a m t", t=PACK))
+        load_table(1)
 
         v = {}
 
@@ -107,8 +113,17 @@ def tile_list_invoice_fraud_screen_kernel(tc, tab_words, tab_scales, offs, w1, w
         nc.vector.tensor_copy(w2[:].rearrange("p a (t m b) -> p a m t b", t=PACK, b=2),
                               w2_raw[:].rearrange("p a (m t b) -> p a m t b", t=PACK, b=2))
         gather(0, 1)
-        load_w1(0)
-        load_w1(1)
+        w1_last = [placed([P, PACK, H // 2], F32, "w1_last%d" % u, TAB0_AT + 1024 + 4096 * u) for u in range(2)]
+        for u in range(2):
+            load_w1(w1_last[u], 1, slice(H // 2 * u, H // 2 * (u + 1)))
+        w3_raw = placed([P, PASSES, H], I32, "w3_raw", TAB0_AT + 1024 + 8192)
+        nc.sync.dma_start(w3_raw[:], w3_words.rearrange("a p c i -> p a (c i)").bitcast(I32))
+        w4_raw = placed([P, PACK, N], F32, "w4_raw", TAB0_AT + TAB_BYTES - 1024)
+        w5 = placed([P, PASSES, 2 * N], U8, "w5", TAB0_AT + 1024 + 12288)
+        prior_sb = [placed([P, NBLK, HALF], F32, "prior0", 1024), placed([P, NBLK, HALF], F32, "prior1", TAB1_AT)]
+        nc.sync.dma_start(w4_raw[:], w4.rearrange("(p j) n -> p j n", j=PACK))
+        nc.sync.dma_start(w5[:].bitcast(I32), w5_words.rearrange("a p c -> p a c").bitcast(I32))
+        load_prior(0)
 
         def moving(a, s):
             return v[a, s][:].bitcast(FP8X4), planes[:, a, HALF * s:HALF * (s + 1)]
@@ -117,109 +132,93 @@ def tile_list_invoice_fraud_screen_kernel(tc, tab_words, tab_scales, offs, w1, w
             return planes[:, a, first + P * block:first + P * (block + 1)]
 
         def mm(acc, lhsT, lhsT_scale, rhs, start, stop):
-            nc.tensor.matmul_mx(out=acc[:], lhsT=lhsT, lhsT_scale=lhsT_scale, rhs=rhs[0], rhs_scale=rhs[1], start=start, stop=stop)
+            nc.tensor.matmul_mx(out=acc, lhsT=lhsT, lhsT_scale=lhsT_scale, rhs=rhs[0], rhs_scale=rhs[1], start=start, stop=stop)
 
         w1q = [held([P, H], U32, "w1q%d" % a) for a in range(PASSES)]
         w1_sc = [held([P, H], U8, "w1_sc%d" % a) for a in range(PASSES)]
+        w1g = [held([P, PACK, P, PACK], BF16, "w1g%d" % a) for a in range(PASSES)]
 
-        def mm_c(acc, a, s, t):
+        def round_w1(a, raw, m0, scalar_m):
+            src = raw[:].rearrange("p j (m t) -> p m t j", t=PACK)
+            count = src.shape[1]
+            dst = w1g[a][:].rearrange("p t m j -> p m t j")[:, m0:m0 + count]
+            nc.scalar.activation(dst[:, :scalar_m], src[:, :scalar_m], ACT.Copy, scale=-1.0)
+            if scalar_m < count:
+                nc.vector.tensor_scalar(dst[:, scalar_m:], src[:, scalar_m:], -1.0, None, ALU.mult)
+
+        def quant_w1(a, t0, t1):
+            cols = slice(P * t0, P * t1)
+            nc.vector.quantize_mx(out=w1q[a][:, cols].bitcast(FP8X4), scales=w1_sc[a][:, cols],
+                                  in_=w1g[a][:, t0:t1].rearrange("p t m j -> p (t m j)"))
+
+        diff = {(s, t): bank() for s in range(HALVES) for t in range(PACK)}
+
+        def pass_w2(a, s):
+            for t in range(PACK):
+                mm(diff[s, t][:], w2[:, a, 2 * P * t:2 * P * (t + 1)].bitcast(FP4X4), plane(a, SC_W2, t), moving(a, s), a == 0, False)
+
+        def pass_w1(a, s, t):
             cols = slice(P * t, P * (t + 1))
-            mm(acc, w3[:, a, cols].bitcast(FP8X4), plane(a, SC_W3, t), moving(a, s), a == 0, a == 1)
+            mm(diff[s, t][:], w1q[a][:, cols].bitcast(FP8X4), w1_sc[a][:, cols], moving(a, s), False, a == 1)
 
-        def mm_b(acc, a, s, t):
-            mm(acc, w2[:, a, 2 * P * t:2 * P * (t + 1)].bitcast(FP4X4), plane(a, SC_W2, t), moving(a, s), a == 0, False)
-
-        def mm_a(acc, a, s, t):
-            cols = slice(P * t, P * (t + 1))
-            mm(acc, w1q[a][:, cols].bitcast(FP8X4), w1_sc[a][:, cols], moving(a, s), False, a == 1)
-
-        def quant_w1(a):
-            grouped = held([P, PACK, P, PACK], BF16, "w1g%d" % a)
-            dst = grouped[:].rearrange("p t m j -> p m t j")
-            src = w1_raw[a][:].rearrange("p j (m t) -> p m t j", t=PACK)
-            nc.scalar.activation(dst[:, :W1_SCALAR_M], src[:, :W1_SCALAR_M], ACT.Copy, scale=-1.0)
-            nc.vector.tensor_scalar(dst[:, W1_SCALAR_M:], src[:, W1_SCALAR_M:], -1.0, None, ALU.mult)
-            nc.vector.quantize_mx(out=w1q[a][:].bitcast(FP8X4), scales=w1_sc[a][:], in_=grouped[:].rearrange("p t m j -> p (t m j)"))
+        for s in range(HALVES):
+            pass_w2(0, s)
+        round_w1(0, w1_first, 0, W1_SCALAR_M)
+        quant_w1(0, 0, PACK)
+        for s in range(HALVES):
+            for t in range(PACK):
+                pass_w1(0, s, t)
+        gather(1, 0)
+        pass_w2(1, 0)
+        gather(1, 1)
+        load_prior(1)
+        round_w1(1, w1_last[0], 0, P // 2)
+        round_w1(1, w1_last[1], P // 2, W1_LAST_SCALAR_M)
+        for t in range(PACK):
+            quant_w1(1, t, t + 1)
+        w3 = held([P, PASSES, H], I32, "w3")
+        nc.vector.tensor_copy(w3[:].rearrange("p a (t m) -> p a m t", t=PACK), w3_raw[:].rearrange("p a (m t) -> p a m t", t=PACK))
 
         h = [held([P, PACK, HALF], F32, "h%d" % s) for s in range(HALVES)]
+        hg = [held([P, HALF, PACK], BF16, "hg%d" % s) for s in range(HALVES)]
         hq = held([P, S], U32, "hq")
         h_sc = held([P, S], U8, "h_sc")
         out1_v = out_1.rearrange("(p t) j -> p t j", t=PACK)
         out2_v = out_2[0].rearrange("p m i -> p (m i)").bitcast(I32)
+        mag = {}
 
-        def finish_slice(s, t, diff, third):
-            mag = ring.tile([P, HALF], F32, name="mag")
-            nc.scalar.activation(mag[:], diff[:], ACT.Abs)
-            nc.vector.tensor_tensor(h[s][:, t, :], mag[:], third[:], ALU.add)
+        def close_diff(s):
+            for t in range(PACK):
+                pass_w1(1, s, t)
+                mag[s, t] = held([P, HALF], F32, "mag%d%d" % (s, t))
+                nc.scalar.activation(mag[s, t][:], diff[s, t][:], ACT.Abs)
+
+        def add_third(s, t):
+            acc = bank()
+            for a in range(PASSES):
+                mm(acc[:], w3[:, a, P * t:P * (t + 1)].bitcast(FP8X4), plane(a, SC_W3, t), moving(a, s), a == 0, a == 1)
+            nc.vector.tensor_tensor(h[s][:, t, :], mag[s, t][:], acc[:], ALU.add)
             if t % 2 == 1:
                 nc.sync.dma_start(out1_v[:, t - 1:t + 1, HALF * s:HALF * (s + 1)], h[s][:, t - 1:t + 1, :])
 
+        def round_h(s, j0, j1):
+            nc.scalar.copy(hg[s][:, j0:j1, :].rearrange("p (c i) t -> p c t i", i=4),
+                           h[s][:, :, j0:j1].rearrange("p t (c i) -> p c t i", i=4))
+
         def quant_h(s):
-            grouped = held([P, HALF, PACK], BF16, "hg%d" % s)
-            dst = grouped[:].rearrange("p (c i) t -> p c t i", i=4)
-            src = h[s][:].rearrange("p t (c i) -> p c t i", i=4)
-            cut = H_SCALAR_COLS[s] // 4
-            for c0 in range(0, cut, 32):
-                c1 = min(cut, c0 + 32)
-                nc.scalar.activation(dst[:, c0:c1], src[:, c0:c1], ACT.Copy)
-            if cut < HALF // 4:
-                nc.vector.tensor_copy(dst[:, cut:], src[:, cut:])
             cols = slice(HALF * s, HALF * (s + 1))
-            nc.vector.quantize_mx(out=hq[:, cols].bitcast(FP8X4), scales=h_sc[:, cols], in_=grouped[:].rearrange("p c t -> p (c t)"))
+            nc.vector.quantize_mx(out=hq[:, cols].bitcast(FP8X4), scales=h_sc[:, cols], in_=hg[s][:].rearrange("p c t -> p (c t)"))
             nc.sync.dma_start(out2_v[:, cols], hq[:, cols].bitcast(I32))
-
-        pairs = [(bank(), bank()) for t in range(PACK)]
-        diff = [pair[0] for pair in pairs]
-        third = [pair[1] for pair in pairs]
-        for t in range(PACK):
-            mm_c(third[t], 0, 0, t)
-        for t in range(PACK):
-            mm_b(diff[t], 0, 0, t)
-        gather(1, 0)
-        for t in range(PACK):
-            mm_c(third[t], 1, 0, t)
-        for t in range(PACK):
-            mm_b(diff[t], 1, 0, t)
-        gather(1, 1)
-        w4_raw = again([P, PACK, N], F32, "w4_raw", 4 * T + 8192)
-        w5 = again([P, PASSES, 2 * N], U8, "w5", 4 * T)
-        nc.sync.dma_start(w5[:].bitcast(I32), w5_words.rearrange("a p c -> p a c").bitcast(I32))
-        nc.sync.dma_start(w4_raw[:], w4.rearrange("(p j) n -> p j n", j=PACK))
-        prior_sb = [again([P, NBLK, HALF], F32, "prior0", 4 * T + 2048), again([P, NBLK, HALF], F32, "prior1", 0)]
-
-        def load_prior(s):
-            nc.sync.dma_start(prior_sb[s][:], prior[:, HALF * s:HALF * (s + 1)].rearrange("(b p) j -> p b j", p=P))
-
-        load_prior(0)
-        quant_w1(0)
-        load_prior(1)
-        for t in range(PACK):
-            mm_a(diff[t], 0, 0, t)
-        quant_w1(1)
-        for t in range(PACK):
-            mm_a(diff[t], 1, 0, t)
-            finish_slice(0, t, diff[t], third[t])
 
         w4g = held([P, N, PACK], BF16, "w4g")
         w4q = held([P, N], U32, "w4q")
         w4_sc = held([P, N], U8, "w4_sc")
 
         def quant_w4():
-            nc.scalar.activation(w4g[:].rearrange("p (c i) j -> p c j i", i=4), w4_raw[:].rearrange("p j (c i) -> p c j i", i=4), ACT.Copy)
+            nc.vector.tensor_copy(w4g[:].rearrange("p (c i) j -> p c j i", i=4), w4_raw[:].rearrange("p j (c i) -> p c j i", i=4))
             flat = w4g[:].rearrange("p n j -> p (n j)")
-            for n0, n1 in ((0, 256), (256, 384)):
+            for n0, n1 in ((0, 256), (256, N)):
                 nc.vector.quantize_mx(out=w4q[:, n0:n1].bitcast(FP8X4), scales=w4_sc[:, n0:n1], in_=flat[:, 4 * n0:4 * n1])
-
-        def second_slice(t):
-            dif = bank()
-            thi = bank()
-            for a in range(PASSES):
-                mm_b(dif, a, 1, t)
-            for a in range(PASSES):
-                mm_a(dif, a, 1, t)
-            for a in range(PASSES):
-                mm_c(thi, a, 1, t)
-            finish_slice(1, t, dif, thi)
 
         base = {}
 
@@ -227,8 +226,7 @@ def tile_list_invoice_fraud_screen_kernel(tc, tab_words, tab_scales, offs, w1, w
             for b in range(NBLK):
                 acc = bank()
                 for a in range(PASSES):
-                    mm(acc, w5[:, a, 2 * P * b:2 * P * (b + 1)].bitcast(FP4X4), plane(a, SC_W5, b),
-                       moving(a, s), a == 0, a == 1)
+                    mm(acc[:], w5[:, a, 2 * P * b:2 * P * (b + 1)].bitcast(FP4X4), plane(a, SC_W5, b), moving(a, s), a == 0, a == 1)
                 base[s, b] = held([P, HALF], F32, "base%d%d" % (s, b))
                 nc.vector.tensor_tensor(base[s, b][:], prior_sb[s][:, b, :], acc[:], ALU.add)
 
@@ -236,24 +234,30 @@ def tile_list_invoice_fraud_screen_kernel(tc, tab_words, tab_scales, offs, w1, w
             cols = slice(HALF * s, HALF * (s + 1))
             for b in range(NBLK):
                 acc = bank()
-                mm(acc, w4q[:, P * b:P * (b + 1)].bitcast(FP8X4), w4_sc[:, P * b:P * (b + 1)],
+                mm(acc[:], w4q[:, P * b:P * (b + 1)].bitcast(FP8X4), w4_sc[:, P * b:P * (b + 1)],
                    (hq[:, cols].bitcast(FP8X4), h_sc[:, cols]), True, True)
-                gate = ring.tile([P, HALF], F32, name="gate")
+                gate = held([P, HALF], F32, "gate%d%d" % (s, b))
                 nc.scalar.activation(gate[:], acc[:], ACT.Silu)
                 y = held([P, HALF], F32, "y%d%d" % (s, b))
                 nc.vector.tensor_tensor(y[:], gate[:], base[s, b][:], ALU.add)
                 nc.sync.dma_start(out_0[P * b:P * (b + 1), cols], y[:])
 
-        second_slice(0)
+        close_diff(0)
+        for t in range(PACK):
+            add_third(0, t)
+        pass_w2(1, 1)
+        close_diff(1)
         quant_w4()
+        for j0 in range(0, HALF, 128):
+            round_h(0, j0, j0 + 128)
         quant_h(0)
-        direct(0)
-        second_slice(1)
-        second_slice(2)
-        scores(0)
-        second_slice(3)
-        direct(1)
+        for t in range(PACK):
+            add_third(1, t)
+        for j0 in range(0, HALF, 256):
+            round_h(1, j0, j0 + 256)
         quant_h(1)
         for q in range(QUADS):
             nc.sync.dma_start(out_3[0, 4 * q:4 * q + 4, :].bitcast(I32), h_sc[32 * q:32 * q + 4, :].bitcast(I32))
-        scores(1)
+        for s in range(HALVES):
+            direct(s)
+            scores(s)

@@ -201,9 +201,12 @@ def tile_list_invoice_fraud_screen_kernel(tc, tab_words, tab_scales, offs, w1, w
             if t % 2 == 1:
                 nc.sync.dma_start(out1_v[:, t - 1:t + 1, HALF * s:HALF * (s + 1)], h[s][:, t - 1:t + 1, :])
 
-        def round_h(s, j0, j1):
-            nc.scalar.copy(hg[s][:, j0:j1, :].rearrange("p (c i) t -> p c t i", i=4),
-                           h[s][:, :, j0:j1].rearrange("p t (c i) -> p c t i", i=4))
+        def round_h(s):
+            dst = hg[s][:].rearrange("p (c i) t -> p c t i", i=4)
+            src = h[s][:].rearrange("p t (c i) -> p c t i", i=4)
+            for c0, c1 in ((0, 40), (40, 80)):
+                nc.scalar.copy(dst[:, c0:c1], src[:, c0:c1])
+            nc.gpsimd.tensor_scalar(hg[s][:, 320:, :], h[s][:, :, 320:].rearrange("p t j -> p j t"), 1.0, 0.0, ALU.mult, ALU.add)
 
         def quant_h(s):
             cols = slice(HALF * s, HALF * (s + 1))
@@ -215,7 +218,7 @@ def tile_list_invoice_fraud_screen_kernel(tc, tab_words, tab_scales, offs, w1, w
         w4_sc = held([P, N], U8, "w4_sc")
 
         def quant_w4():
-            nc.vector.tensor_copy(w4g[:].rearrange("p (c i) j -> p c j i", i=4), w4_raw[:].rearrange("p j (c i) -> p c j i", i=4))
+            nc.gpsimd.tensor_scalar(w4g[:], w4_raw[:].rearrange("p j n -> p n j"), 1.0, 0.0, ALU.mult, ALU.add)
             flat = w4g[:].rearrange("p n j -> p (n j)")
             for n0, n1 in ((0, 256), (256, N)):
                 nc.vector.quantize_mx(out=w4q[:, n0:n1].bitcast(FP8X4), scales=w4_sc[:, n0:n1], in_=flat[:, 4 * n0:4 * n1])
@@ -239,7 +242,8 @@ def tile_list_invoice_fraud_screen_kernel(tc, tab_words, tab_scales, offs, w1, w
                 gate = held([P, HALF], F32, "gate%d%d" % (s, b))
                 nc.scalar.activation(gate[:], acc[:], ACT.Silu)
                 y = held([P, HALF], F32, "y%d%d" % (s, b))
-                nc.vector.tensor_tensor(y[:], gate[:], base[s, b][:], ALU.add)
+                adder = nc.gpsimd if s == 0 and b != 1 else nc.vector
+                adder.tensor_tensor(y[:], gate[:], base[s, b][:], ALU.add)
                 nc.sync.dma_start(out_0[P * b:P * (b + 1), cols], y[:])
 
         close_diff(0)
@@ -248,13 +252,11 @@ def tile_list_invoice_fraud_screen_kernel(tc, tab_words, tab_scales, offs, w1, w
         pass_w2(1, 1)
         close_diff(1)
         quant_w4()
-        for j0 in range(0, HALF, 128):
-            round_h(0, j0, j0 + 128)
+        round_h(0)
         quant_h(0)
         for t in range(PACK):
             add_third(1, t)
-        for j0 in range(0, HALF, 256):
-            round_h(1, j0, j0 + 256)
+        round_h(1)
         quant_h(1)
         for q in range(QUADS):
             nc.sync.dma_start(out_3[0, 4 * q:4 * q + 4, :].bitcast(I32), h_sc[32 * q:32 * q + 4, :].bitcast(I32))

@@ -23,15 +23,12 @@ PASSES = K // K_PASS
 HALF = 512
 HALVES = S // HALF
 NBLK = N // P
-QUADS = 4
 BANKS = 8
 ROW0 = 96
 SC_W2, SC_W3, SC_W5, SC_COLS = S, S + H, S + 2 * H, S + 2 * H + N
 TAB_BYTES = 4 * T
 TAB0_AT = 6144
 TAB1_AT = TAB0_AT + TAB_BYTES + 6144
-W1_SCALAR_M = 48
-W1_LAST_SCALAR_M = 24
 
 
 def tile_list_invoice_fraud_screen_kernel(tc, tab_words, tab_scales, offs, w1, w2_words, w2_scales,
@@ -75,8 +72,8 @@ def tile_list_invoice_fraud_screen_kernel(tc, tab_words, tab_scales, offs, w1, w
         def load_table(a):
             nc.sync.dma_start(tab[a][:], tab_words[a].rearrange("p t i -> p (t i)").bitcast(I32))
 
-        def load_w1(dst, a, cols):
-            nc.sync.dma_start(dst[:], w1[K_PASS * a:K_PASS * (a + 1), cols].rearrange("(p j) c -> p j c", j=PACK))
+        def load_w1(dst, a):
+            nc.sync.dma_start(dst[:], w1[K_PASS * a:K_PASS * (a + 1), :].rearrange("(p j) c -> p j c", j=PACK))
 
         def load_prior(s):
             nc.sync.dma_start(prior_sb[s][:], prior[:, HALF * s:HALF * (s + 1)].rearrange("(b p) j -> p b j", p=P))
@@ -91,11 +88,11 @@ def tile_list_invoice_fraud_screen_kernel(tc, tab_words, tab_scales, offs, w1, w
         load_table(0)
         nc.sync.dma_start(w2_raw[:].bitcast(I32), w2_words.rearrange("a p c -> p a c").bitcast(I32))
         w1_first = held([P, PACK, H], F32, "w1_first")
-        load_w1(w1_first, 0, slice(0, H))
+        load_w1(w1_first, 0)
 
         v_sc = placed([P, S], U8, "v_sc", TAB1_AT)
-        nc.vector.tensor_copy(rows[:, SC_W2:SC_W5].rearrange("p (w t m) -> p w m t", w=2, t=PACK),
-                              w23_sc_raw[:].rearrange("p w (m t) -> p w m t", t=PACK))
+        nc.vector.tensor_copy(rows[:, SC_W2:SC_W5].rearrange("p (w t c i) -> p w c t i", w=2, t=PACK, i=16),
+                              w23_sc_raw[:].rearrange("p w (c i t) -> p w c t i", t=PACK, i=16))
         nc.vector.tensor_copy(v_sc[:], tab_sc[:].indirect(offsets[:]))
         nc.vector.tensor_copy(rows[:, :S].bitcast(I32), v_sc[:].bitcast(I32))
         for q in (0, 2, 1, 3):
@@ -110,12 +107,11 @@ def tile_list_invoice_fraud_screen_kernel(tc, tab_words, tab_scales, offs, w1, w
 
         gather(0, 0)
         w2 = held([P, PASSES, 2 * H], U8, "w2")
-        nc.vector.tensor_copy(w2[:].rearrange("p a (t m b) -> p a m t b", t=PACK, b=2),
-                              w2_raw[:].rearrange("p a (m t b) -> p a m t b", t=PACK, b=2))
+        nc.vector.tensor_copy(w2[:].bitcast(U16).rearrange("p a (t c i) -> p a c t i", t=PACK, i=8),
+                              w2_raw[:].bitcast(U16).rearrange("p a (c i t) -> p a c t i", t=PACK, i=8))
         gather(0, 1)
-        w1_last = [placed([P, PACK, H // 2], F32, "w1_last%d" % u, TAB0_AT + 1024 + 4096 * u) for u in range(2)]
-        for u in range(2):
-            load_w1(w1_last[u], 1, slice(H // 2 * u, H // 2 * (u + 1)))
+        w1_last = placed([P, PACK, H], F32, "w1_last", TAB0_AT + 1024)
+        load_w1(w1_last, 1)
         w3_raw = placed([P, PASSES, H], I32, "w3_raw", TAB0_AT + 1024 + 8192)
         nc.sync.dma_start(w3_raw[:], w3_words.rearrange("a p c i -> p a (c i)").bitcast(I32))
         w4_raw = placed([P, PACK, N], F32, "w4_raw", TAB0_AT + TAB_BYTES - 1024)
@@ -136,20 +132,16 @@ def tile_list_invoice_fraud_screen_kernel(tc, tab_words, tab_scales, offs, w1, w
 
         w1q = [held([P, H], U32, "w1q%d" % a) for a in range(PASSES)]
         w1_sc = [held([P, H], U8, "w1_sc%d" % a) for a in range(PASSES)]
-        w1g = [held([P, PACK, P, PACK], BF16, "w1g%d" % a) for a in range(PASSES)]
+        w1g = {(a, u): held([P, 2, P, PACK], BF16, "w1g%d%d" % (a, u)) for a in range(PASSES) for u in range(2)}
 
-        def round_w1(a, raw, m0, scalar_m):
+        def prepare_w1(a, raw):
             src = raw[:].rearrange("p j (m t) -> p m t j", t=PACK)
-            count = src.shape[1]
-            dst = w1g[a][:].rearrange("p t m j -> p m t j")[:, m0:m0 + count]
-            nc.scalar.activation(dst[:, :scalar_m], src[:, :scalar_m], ACT.Copy, scale=-1.0)
-            if scalar_m < count:
-                nc.vector.tensor_scalar(dst[:, scalar_m:], src[:, scalar_m:], -1.0, None, ALU.mult)
-
-        def quant_w1(a, t0, t1):
-            cols = slice(P * t0, P * t1)
-            nc.vector.quantize_mx(out=w1q[a][:, cols].bitcast(FP8X4), scales=w1_sc[a][:, cols],
-                                  in_=w1g[a][:, t0:t1].rearrange("p t m j -> p (t m j)"))
+            nc.vector.tensor_scalar(w1g[a, 0][:].rearrange("p t m j -> p m t j"), src[:, :, 0:2, :], -1.0, None, ALU.mult)
+            nc.scalar.activation(w1g[a, 1][:].rearrange("p t m j -> p m t j"), src[:, :, 2:4, :], ACT.Copy, scale=-1.0)
+            for u in range(2):
+                cols = slice(2 * P * u, 2 * P * (u + 1))
+                nc.vector.quantize_mx(out=w1q[a][:, cols].bitcast(FP8X4), scales=w1_sc[a][:, cols],
+                                      in_=w1g[a, u][:].rearrange("p t m j -> p (t m j)"))
 
         diff = {(s, t): bank() for s in range(HALVES) for t in range(PACK)}
 
@@ -163,8 +155,7 @@ def tile_list_invoice_fraud_screen_kernel(tc, tab_words, tab_scales, offs, w1, w
 
         for s in range(HALVES):
             pass_w2(0, s)
-        round_w1(0, w1_first, 0, W1_SCALAR_M)
-        quant_w1(0, 0, PACK)
+        prepare_w1(0, w1_first)
         for s in range(HALVES):
             for t in range(PACK):
                 pass_w1(0, s, t)
@@ -172,12 +163,10 @@ def tile_list_invoice_fraud_screen_kernel(tc, tab_words, tab_scales, offs, w1, w
         pass_w2(1, 0)
         gather(1, 1)
         load_prior(1)
-        round_w1(1, w1_last[0], 0, P // 2)
-        round_w1(1, w1_last[1], P // 2, W1_LAST_SCALAR_M)
-        for t in range(PACK):
-            quant_w1(1, t, t + 1)
+        prepare_w1(1, w1_last)
         w3 = held([P, PASSES, H], I32, "w3")
-        nc.vector.tensor_copy(w3[:].rearrange("p a (t m) -> p a m t", t=PACK), w3_raw[:].rearrange("p a (m t) -> p a m t", t=PACK))
+        nc.vector.tensor_copy(w3[:].rearrange("p a (t c i) -> p a c t i", t=PACK, i=4),
+                              w3_raw[:].rearrange("p a (c i t) -> p a c t i", t=PACK, i=4))
 
         h = [held([P, PACK, HALF], F32, "h%d" % s) for s in range(HALVES)]
         hg = [held([P, HALF, PACK], BF16, "hg%d" % s) for s in range(HALVES)]
@@ -258,7 +247,7 @@ def tile_list_invoice_fraud_screen_kernel(tc, tab_words, tab_scales, offs, w1, w
             add_third(1, t)
         round_h(1)
         quant_h(1)
-        for q in range(QUADS):
+        for q in range(4):
             nc.sync.dma_start(out_3[0, 4 * q:4 * q + 4, :].bitcast(I32), h_sc[32 * q:32 * q + 4, :].bitcast(I32))
         for s in range(HALVES):
             direct(s)

@@ -72,8 +72,8 @@ def tile_list_invoice_fraud_screen_kernel(tc, tab_words, tab_scales, offs, w1, w
         def load_table(a):
             nc.sync.dma_start(tab[a][:], tab_words[a].rearrange("p t i -> p (t i)").bitcast(I32))
 
-        def load_w1(dst, a):
-            nc.sync.dma_start(dst[:], w1[K_PASS * a:K_PASS * (a + 1), :].rearrange("(p j) c -> p j c", j=PACK))
+        def load_w1(dst, a, cols):
+            nc.sync.dma_start(dst[:], w1[K_PASS * a:K_PASS * (a + 1), cols].rearrange("(p j) c -> p j c", j=PACK))
 
         def load_prior(s):
             nc.sync.dma_start(prior_sb[s][:], prior[:, HALF * s:HALF * (s + 1)].rearrange("(b p) j -> p b j", p=P))
@@ -88,7 +88,7 @@ def tile_list_invoice_fraud_screen_kernel(tc, tab_words, tab_scales, offs, w1, w
         load_table(0)
         nc.sync.dma_start(w2_raw[:].bitcast(I32), w2_words.rearrange("a p c -> p a c").bitcast(I32))
         w1_first = held([P, PACK, H], F32, "w1_first")
-        load_w1(w1_first, 0)
+        load_w1(w1_first, 0, slice(0, H))
 
         v_sc = placed([P, S], U8, "v_sc", TAB1_AT)
         nc.vector.tensor_copy(rows[:, SC_W2:SC_W5].rearrange("p (w t c i) -> p w c t i", w=2, t=PACK, i=16),
@@ -110,8 +110,9 @@ def tile_list_invoice_fraud_screen_kernel(tc, tab_words, tab_scales, offs, w1, w
         nc.vector.tensor_copy(w2[:].bitcast(U16).rearrange("p a (t c i) -> p a c t i", t=PACK, i=8),
                               w2_raw[:].bitcast(U16).rearrange("p a (c i t) -> p a c t i", t=PACK, i=8))
         gather(0, 1)
-        w1_last = placed([P, PACK, H], F32, "w1_last", TAB0_AT + 1024)
-        load_w1(w1_last, 1)
+        w1_last = [placed([P, PACK, H // 2], F32, "w1_last%d" % u, TAB0_AT + 1024 + 4096 * u) for u in range(2)]
+        for u in range(2):
+            load_w1(w1_last[u], 1, slice(H // 2 * u, H // 2 * (u + 1)))
         w3_raw = placed([P, PASSES, H], I32, "w3_raw", TAB0_AT + 1024 + 8192)
         nc.sync.dma_start(w3_raw[:], w3_words.rearrange("a p c i -> p a (c i)").bitcast(I32))
         w4_raw = placed([P, PACK, N], F32, "w4_raw", TAB0_AT + TAB_BYTES - 1024)
@@ -132,16 +133,18 @@ def tile_list_invoice_fraud_screen_kernel(tc, tab_words, tab_scales, offs, w1, w
 
         w1q = [held([P, H], U32, "w1q%d" % a) for a in range(PASSES)]
         w1_sc = [held([P, H], U8, "w1_sc%d" % a) for a in range(PASSES)]
-        w1g = {(a, u): held([P, 2, P, PACK], BF16, "w1g%d%d" % (a, u)) for a in range(PASSES) for u in range(2)}
+        w1g = {(a, u): held([P, PACK, P // 2, PACK], BF16, "w1g%d%d" % (a, u)) for a in range(PASSES) for u in range(2)}
 
-        def prepare_w1(a, raw):
-            src = raw[:].rearrange("p j (m t) -> p m t j", t=PACK)
-            nc.vector.tensor_scalar(w1g[a, 0][:].rearrange("p t m j -> p m t j"), src[:, :, 0:2, :], -1.0, None, ALU.mult)
-            nc.scalar.activation(w1g[a, 1][:].rearrange("p t m j -> p m t j"), src[:, :, 2:4, :], ACT.Copy, scale=-1.0)
-            for u in range(2):
-                cols = slice(2 * P * u, 2 * P * (u + 1))
-                nc.vector.quantize_mx(out=w1q[a][:, cols].bitcast(FP8X4), scales=w1_sc[a][:, cols],
-                                      in_=w1g[a, u][:].rearrange("p t m j -> p (t m j)"))
+        def prepare_w1(a, halves):
+            dst = [w1g[a, u][:].rearrange("p t m j -> p m t j") for u in range(2)]
+            src = [half.rearrange("p j (m t) -> p m t j", t=PACK) for half in halves]
+            nc.scalar.activation(dst[0], src[0], ACT.Copy, scale=-1.0)
+            nc.vector.tensor_scalar(dst[1], src[1], -1.0, None, ALU.mult)
+            for t in range(PACK):
+                for u in range(2):
+                    cols = slice(P * t + P // 2 * u, P * t + P // 2 * (u + 1))
+                    nc.vector.quantize_mx(out=w1q[a][:, cols].bitcast(FP8X4), scales=w1_sc[a][:, cols],
+                                          in_=w1g[a, u][:, t].rearrange("p m j -> p (m j)"))
 
         diff = {(s, t): bank() for s in range(HALVES) for t in range(PACK)}
 
@@ -155,7 +158,7 @@ def tile_list_invoice_fraud_screen_kernel(tc, tab_words, tab_scales, offs, w1, w
 
         for s in range(HALVES):
             pass_w2(0, s)
-        prepare_w1(0, w1_first)
+        prepare_w1(0, [w1_first[:, :, :H // 2], w1_first[:, :, H // 2:]])
         for s in range(HALVES):
             for t in range(PACK):
                 pass_w1(0, s, t)
@@ -163,7 +166,7 @@ def tile_list_invoice_fraud_screen_kernel(tc, tab_words, tab_scales, offs, w1, w
         pass_w2(1, 0)
         gather(1, 1)
         load_prior(1)
-        prepare_w1(1, w1_last)
+        prepare_w1(1, [w1_last[0][:], w1_last[1][:]])
         w3 = held([P, PASSES, H], I32, "w3")
         nc.vector.tensor_copy(w3[:].rearrange("p a (t c i) -> p a c t i", t=PACK, i=4),
                               w3_raw[:].rearrange("p a (c i t) -> p a c t i", t=PACK, i=4))

@@ -27,6 +27,7 @@ BANKS = 8
 ROW0 = 96
 SC_W2, SC_W3, SC_W5, SC_COLS = S, S + H, S + 2 * H, S + 2 * H + N
 TAB_BYTES = 4 * T
+WARM_PASSES = 4
 TAB0_AT = 6144
 TAB1_AT = TAB0_AT + TAB_BYTES + 6144
 
@@ -81,12 +82,12 @@ def tile_list_invoice_fraud_screen_kernel(tc, tab_words, tab_scales, offs, w1, w
         tab = [placed([P, T], I32, "tab0", TAB0_AT), placed([P, T], I32, "tab1", TAB1_AT)]
         w2_raw = held([P, PASSES, 2 * H], U8, "w2_raw")
         nc.sync.dma_start(offsets[:], offs)
+        load_rows(tab_sc[ROW0:, :], tab_scales)
+        nc.sync.dma_start(w2_raw[:].bitcast(I32), w2_words.rearrange("a p c -> p a c").bitcast(I32))
         load_rows(w23_sc_raw[ROW0:, 0, :], w2_scales)
         load_rows(w23_sc_raw[ROW0:, 1, :], w3_scales)
-        load_rows(tab_sc[ROW0:, :], tab_scales)
         load_rows(rows[ROW0:, SC_W5:], w5_scales)
         load_table(0)
-        nc.sync.dma_start(w2_raw[:].bitcast(I32), w2_words.rearrange("a p c -> p a c").bitcast(I32))
         w1_first = held([P, PACK, H], F32, "w1_first")
         load_w1(w1_first, 0, slice(0, H))
 
@@ -156,6 +157,9 @@ def tile_list_invoice_fraud_screen_kernel(tc, tab_words, tab_scales, offs, w1, w
             cols = slice(P * t, P * (t + 1))
             mm(diff[s, t][:], w1q[a][:, cols].bitcast(FP8X4), w1_sc[a][:, cols], moving(a, s), False, a == 1)
 
+        for i in range(WARM_PASSES):
+            mm(diff[1, PACK - 1][:], w2[:, 0, :2 * P].bitcast(FP4X4), rows[:, SC_W2:SC_W2 + P],
+               (v[0, 0][:].bitcast(FP8X4), rows[:, :HALF]), True, True)
         for s in range(HALVES):
             pass_w2(0, s)
         prepare_w1(0, [w1_first[:, :, :H // 2], w1_first[:, :, H // 2:]])

@@ -28,7 +28,7 @@ ROW0 = 96
 SC_W2, SC_W3, SC_W5, SC_COLS = S, S + H, S + 2 * H, S + 2 * H + N
 TAB_BYTES = 4 * T
 WARM_PASSES = 4
-TAB0_AT = 6144
+TAB0_AT = 12288
 TAB1_AT = TAB0_AT + TAB_BYTES + 6144
 
 
@@ -76,9 +76,6 @@ def tile_list_invoice_fraud_screen_kernel(tc, tab_words, tab_scales, offs, w1, w
         def load_w1(dst, a, cols):
             nc.sync.dma_start(dst[:], w1[K_PASS * a:K_PASS * (a + 1), cols].rearrange("(p j) c -> p j c", j=PACK))
 
-        def load_prior(s):
-            nc.sync.dma_start(prior_sb[s][:], prior[:, HALF * s:HALF * (s + 1)].rearrange("(b p) j -> p b j", p=P))
-
         tab = [placed([P, T], I32, "tab0", TAB0_AT), placed([P, T], I32, "tab1", TAB1_AT)]
         w2_raw = held([P, PASSES, 2 * H], U8, "w2_raw")
         nc.sync.dma_start(offsets[:], offs)
@@ -118,10 +115,10 @@ def tile_list_invoice_fraud_screen_kernel(tc, tab_words, tab_scales, offs, w1, w
         nc.sync.dma_start(w3_raw[:], w3_words.rearrange("a p c i -> p a (c i)").bitcast(I32))
         w4_raw = placed([P, PACK, N], F32, "w4_raw", TAB0_AT + TAB_BYTES - 1024)
         w5 = placed([P, PASSES, 2 * N], U8, "w5", TAB0_AT + 1024 + 12288)
-        prior_sb = [placed([P, NBLK, HALF], F32, "prior0", 1024), placed([P, NBLK, HALF], F32, "prior1", TAB1_AT)]
+        prior_sb = placed([P, NBLK, S], F32, "prior_sb", TAB0_AT + 1024 - 4 * NBLK * S)
         nc.sync.dma_start(w4_raw[:], w4.rearrange("(p j) n -> p j n", j=PACK))
         nc.sync.dma_start(w5[:].bitcast(I32), w5_words.rearrange("a p c -> p a c").bitcast(I32))
-        load_prior(0)
+        nc.sync.dma_start(prior_sb[:], prior.rearrange("(b p) j -> p b j", p=P))
 
         def moving(a, s):
             return v[a, s][:].bitcast(FP8X4), planes[:, a, HALF * s:HALF * (s + 1)]
@@ -169,7 +166,6 @@ def tile_list_invoice_fraud_screen_kernel(tc, tab_words, tab_scales, offs, w1, w
         gather(1, 0)
         pass_w2(1, 0)
         gather(1, 1)
-        load_prior(1)
         prepare_w1(1, [w1_last[0][:], w1_last[1][:]])
         w3 = held([P, PASSES, H], I32, "w3")
         nc.vector.tensor_copy(w3[:].rearrange("p a (t c i) -> p a c t i", t=PACK, i=4),
@@ -194,8 +190,8 @@ def tile_list_invoice_fraud_screen_kernel(tc, tab_words, tab_scales, offs, w1, w
             for a in range(PASSES):
                 mm(acc[:], w3[:, a, P * t:P * (t + 1)].bitcast(FP8X4), plane(a, SC_W3, t), moving(a, s), a == 0, a == 1)
             nc.vector.tensor_tensor(h[s][:, t, :], mag[s, t][:], acc[:], ALU.add)
-            if t % 2 == 1:
-                nc.sync.dma_start(out1_v[:, t - 1:t + 1, HALF * s:HALF * (s + 1)], h[s][:, t - 1:t + 1, :])
+            if t == PACK - 1:
+                nc.sync.dma_start(out1_v[:, :, HALF * s:HALF * (s + 1)], h[s][:])
 
         def round_h(s):
             dst = hg[s][:].rearrange("p (c i) t -> p c t i", i=4)
@@ -207,7 +203,6 @@ def tile_list_invoice_fraud_screen_kernel(tc, tab_words, tab_scales, offs, w1, w
         def quant_h(s):
             cols = slice(HALF * s, HALF * (s + 1))
             nc.vector.quantize_mx(out=hq[:, cols].bitcast(FP8X4), scales=h_sc[:, cols], in_=hg[s][:].rearrange("p c t -> p (c t)"))
-            nc.sync.dma_start(out2_v[:, cols], hq[:, cols].bitcast(I32))
 
         w4g = held([P, N, PACK], BF16, "w4g")
         w4q = held([P, N], U32, "w4q")
@@ -227,7 +222,7 @@ def tile_list_invoice_fraud_screen_kernel(tc, tab_words, tab_scales, offs, w1, w
                 for a in range(PASSES):
                     mm(acc[:], w5[:, a, 2 * P * b:2 * P * (b + 1)].bitcast(FP4X4), plane(a, SC_W5, b), moving(a, s), a == 0, a == 1)
                 base[s, b] = held([P, HALF], F32, "base%d%d" % (s, b))
-                nc.vector.tensor_tensor(base[s, b][:], prior_sb[s][:, b, :], acc[:], ALU.add)
+                nc.vector.tensor_tensor(base[s, b][:], prior_sb[:, b, HALF * s:HALF * (s + 1)], acc[:], ALU.add)
 
         def scores(s):
             cols = slice(HALF * s, HALF * (s + 1))
@@ -254,8 +249,9 @@ def tile_list_invoice_fraud_screen_kernel(tc, tab_words, tab_scales, offs, w1, w
             add_third(1, t)
         round_h(1)
         quant_h(1)
-        for q in range(4):
-            nc.sync.dma_start(out_3[0, 4 * q:4 * q + 4, :].bitcast(I32), h_sc[32 * q:32 * q + 4, :].bitcast(I32))
+        nc.sync.dma_start(out2_v, hq[:].bitcast(I32))
+        for r in range(4):
+            nc.sync.dma_start(out_3[0, r:16:4, :].bitcast(I32), h_sc[r:P:32, :].bitcast(I32))
         for s in range(HALVES):
             direct(s)
             scores(s)

@@ -24,12 +24,14 @@ HALF = 512
 HALVES = S // HALF
 NBLK = N // P
 BANKS = 8
-ROW0 = 96
 SC_W2, SC_W3, SC_W5, SC_COLS = S, S + H, S + 2 * H, S + 2 * H + N
 TAB_BYTES = 4 * T
 WARM_PASSES = 4
 TAB0_AT = 12288
 TAB1_AT = TAB0_AT + TAB_BYTES + 6144
+STAGE_AT = TAB1_AT + TAB_BYTES
+W1_AT = STAGE_AT + 4096 + 512
+W2_RAW_AT = W1_AT + 8192 + 4096
 
 
 def tile_list_invoice_fraud_screen_kernel(tc, tab_words, tab_scales, offs, w1, w2_words, w2_scales,
@@ -54,15 +56,15 @@ def tile_list_invoice_fraud_screen_kernel(tc, tab_words, tab_scales, offs, w1, w
             return psum.tile([P, HALF], F32, name="bank%d" % taken[-1])
 
         offsets = keep.tile([P, S // 16], U16, name="offsets")
-        tab_sc = held([P, T], U8, "tab_sc")
+        tab_sc = placed([P, T], U8, "tab_sc", STAGE_AT)
         w23_sc_raw = held([P, 2, H], U8, "w23_sc_raw")
         rows = held([P, SC_COLS], U8, "rows")
         planes = held([P, PASSES, SC_COLS], U8, "planes")
         warm_in = held([P, 8], F32, "warm_in")
         warm_out = held([P, 8], F32, "warm_out")
 
-        nc.vector.memset(w23_sc_raw[:ROW0].bitcast(I32), 0)
-        nc.vector.memset(tab_sc[:ROW0].bitcast(I32), 0)
+        nc.vector.memset(w23_sc_raw[:].bitcast(I32), 0)
+        nc.vector.memset(tab_sc[:].bitcast(I32), 0)
         nc.gpsimd.memset(warm_in[:], 0.0)
         nc.gpsimd.memset(planes[:].bitcast(I32), 0)
         nc.scalar.activation(warm_out[:], warm_in[:], ACT.Silu)
@@ -77,16 +79,16 @@ def tile_list_invoice_fraud_screen_kernel(tc, tab_words, tab_scales, offs, w1, w
             nc.sync.dma_start(dst[:], w1[K_PASS * a:K_PASS * (a + 1), cols].rearrange("(p j) c -> p j c", j=PACK))
 
         tab = [placed([P, T], I32, "tab0", TAB0_AT), placed([P, T], I32, "tab1", TAB1_AT)]
-        w2_raw = held([P, PASSES, 2 * H], U8, "w2_raw")
+        w2_raw = placed([P, PASSES, 2 * H], U8, "w2_raw", W2_RAW_AT)
         nc.sync.dma_start(offsets[:], offs)
-        load_rows(tab_sc[ROW0:, :], tab_scales)
-        nc.sync.dma_start(w2_raw[:].bitcast(I32), w2_words.rearrange("a p c -> p a c").bitcast(I32))
-        load_rows(w23_sc_raw[ROW0:, 0, :], w2_scales)
-        load_rows(w23_sc_raw[ROW0:, 1, :], w3_scales)
-        load_rows(rows[ROW0:, SC_W5:], w5_scales)
-        load_table(0)
-        w1_first = held([P, PACK, H], F32, "w1_first")
+        w1_first = placed([P, PACK, H], F32, "w1_first", W1_AT)
         load_w1(w1_first, 0, slice(0, H))
+        load_rows(rows[0:P:4, SC_W5:], w5_scales)
+        load_rows(w23_sc_raw[0:P:4, 0, :], w2_scales)
+        load_rows(w23_sc_raw[0:P:4, 1, :], w3_scales)
+        load_rows(tab_sc[0:P:4, :], tab_scales)
+        nc.sync.dma_start(w2_raw[:].bitcast(I32), w2_words.rearrange("a p c -> p a c").bitcast(I32))
+        load_table(0)
 
         v_sc = placed([P, S], U8, "v_sc", TAB1_AT)
         nc.vector.tensor_copy(rows[:, SC_W2:SC_W5].rearrange("p (w t c i) -> p w c t i", w=2, t=PACK, i=16),
@@ -94,7 +96,7 @@ def tile_list_invoice_fraud_screen_kernel(tc, tab_words, tab_scales, offs, w1, w
         nc.vector.tensor_copy(v_sc[:], tab_sc[:].indirect(offsets[:]))
         nc.vector.tensor_copy(rows[:, :S].bitcast(I32), v_sc[:].bitcast(I32))
         for q in (0, 2, 1, 3):
-            nc.sync.dma_start(planes[32 * q:32 * q + 4].bitcast(I32), rows[ROW0 + 8 * q:ROW0 + 8 * q + 8, :].bitcast(I32))
+            nc.sync.dma_start(planes[32 * q:32 * q + 4].bitcast(I32), rows[32 * q:32 * q + 32:4, :].bitcast(I32))
         load_table(1)
 
         v = {}
@@ -103,17 +105,34 @@ def tile_list_invoice_fraud_screen_kernel(tc, tab_words, tab_scales, offs, w1, w
             v[a, s] = held([P, HALF], U32, "v%d%d" % (a, s))
             nc.vector.tensor_copy(v[a, s][:], tab[a][:].bitcast(U32).indirect(offsets[:, 32 * s:32 * (s + 1)]))
 
-        gather(0, 0)
-        w2 = held([P, PASSES, 2 * H], U8, "w2")
+        w1q = [held([P, H], U32, "w1q%d" % a) for a in range(PASSES)]
+        w1_sc = [placed([P, H], U8, "w1_sc0", STAGE_AT + 2048), held([P, H], U8, "w1_sc1")]
+        w1g = {(a, u): held([P, PACK, P // 2, PACK], BF16, "w1g%d%d" % (a, u)) for a, u in ((0, 0), (1, 0), (1, 1))}
+        w1g[0, 1] = placed([P, PACK, P // 2, PACK], BF16, "w1g01", STAGE_AT)
+
+        def prepare_w1(a, halves):
+            dst = [w1g[a, u][:].rearrange("p t m j -> p m t j") for u in range(2)]
+            src = [half.rearrange("p j (m t) -> p m t j", t=PACK) for half in halves]
+            nc.scalar.activation(dst[0], src[0], ACT.Copy, scale=-1.0)
+            nc.vector.tensor_scalar(dst[1], src[1], -1.0, None, ALU.mult)
+            for t in range(PACK):
+                for u in range(2):
+                    cols = slice(P * t + P // 2 * u, P * t + P // 2 * (u + 1))
+                    nc.vector.quantize_mx(out=w1q[a][:, cols].bitcast(FP8X4), scales=w1_sc[a][:, cols],
+                                          in_=w1g[a, u][:, t].rearrange("p m j -> p (m j)"))
+
+        prepare_w1(0, [w1_first[:, :, :H // 2], w1_first[:, :, H // 2:]])
+        w2 = placed([P, PASSES, 2 * H], U8, "w2", STAGE_AT + 2048 + 512)
         nc.vector.tensor_copy(w2[:].bitcast(U16).rearrange("p a (t c i) -> p a c t i", t=PACK, i=8),
                               w2_raw[:].bitcast(U16).rearrange("p a (c i t) -> p a c t i", t=PACK, i=8))
+        gather(0, 0)
         gather(0, 1)
-        w1_last = [placed([P, PACK, H // 2], F32, "w1_last%d" % u, TAB0_AT + 1024 + 4096 * u) for u in range(2)]
+        w1_last = [placed([P, PACK, H // 2], F32, "w1_last%d" % u, W1_AT + 4096 * u) for u in range(2)]
         for u in range(2):
             load_w1(w1_last[u], 1, slice(H // 2 * u, H // 2 * (u + 1)))
-        w3_raw = placed([P, PASSES, H], I32, "w3_raw", TAB0_AT + 1024 + 8192)
+        w3_raw = placed([P, PASSES, H], I32, "w3_raw", W2_RAW_AT + 1024 - 4096)
         nc.sync.dma_start(w3_raw[:], w3_words.rearrange("a p c i -> p a (c i)").bitcast(I32))
-        w4_raw = placed([P, PACK, N], F32, "w4_raw", TAB0_AT + TAB_BYTES - 1024)
+        w4_raw = placed([P, PACK, N], F32, "w4_raw", W2_RAW_AT + 1024)
         w5 = placed([P, PASSES, 2 * N], U8, "w5", TAB0_AT + 1024 + 12288)
         prior_sb = placed([P, NBLK, S], F32, "prior_sb", TAB0_AT + 1024 - 4 * NBLK * S)
         nc.sync.dma_start(w4_raw[:], w4.rearrange("(p j) n -> p j n", j=PACK))
@@ -129,21 +148,6 @@ def tile_list_invoice_fraud_screen_kernel(tc, tab_words, tab_scales, offs, w1, w
         def mm(acc, lhsT, lhsT_scale, rhs, start, stop):
             nc.tensor.matmul_mx(out=acc, lhsT=lhsT, lhsT_scale=lhsT_scale, rhs=rhs[0], rhs_scale=rhs[1], start=start, stop=stop)
 
-        w1q = [held([P, H], U32, "w1q%d" % a) for a in range(PASSES)]
-        w1_sc = [held([P, H], U8, "w1_sc%d" % a) for a in range(PASSES)]
-        w1g = {(a, u): held([P, PACK, P // 2, PACK], BF16, "w1g%d%d" % (a, u)) for a in range(PASSES) for u in range(2)}
-
-        def prepare_w1(a, halves):
-            dst = [w1g[a, u][:].rearrange("p t m j -> p m t j") for u in range(2)]
-            src = [half.rearrange("p j (m t) -> p m t j", t=PACK) for half in halves]
-            nc.scalar.activation(dst[0], src[0], ACT.Copy, scale=-1.0)
-            nc.vector.tensor_scalar(dst[1], src[1], -1.0, None, ALU.mult)
-            for t in range(PACK):
-                for u in range(2):
-                    cols = slice(P * t + P // 2 * u, P * t + P // 2 * (u + 1))
-                    nc.vector.quantize_mx(out=w1q[a][:, cols].bitcast(FP8X4), scales=w1_sc[a][:, cols],
-                                          in_=w1g[a, u][:, t].rearrange("p m j -> p (m j)"))
-
         diff = {(s, t): bank() for s in range(HALVES) for t in range(PACK)}
 
         def pass_w2(a, s):
@@ -156,11 +160,9 @@ def tile_list_invoice_fraud_screen_kernel(tc, tab_words, tab_scales, offs, w1, w
 
         for i in range(WARM_PASSES):
             mm(diff[1, PACK - 1][:], w2[:, 0, :2 * P].bitcast(FP4X4), rows[:, SC_W2:SC_W2 + P],
-               (v[0, 0][:].bitcast(FP8X4), rows[:, :HALF]), True, True)
+               (w1q[0][:].bitcast(FP8X4), w1_sc[0][:]), True, True)
         for s in range(HALVES):
             pass_w2(0, s)
-        prepare_w1(0, [w1_first[:, :, :H // 2], w1_first[:, :, H // 2:]])
-        for s in range(HALVES):
             for t in range(PACK):
                 pass_w1(0, s, t)
         gather(1, 0)

@@ -26,7 +26,6 @@ NBLK = N // P
 BANKS = 8
 SC_W2, SC_W3, SC_W5, SC_COLS = S, S + H, S + 2 * H, S + 2 * H + N
 TAB_BYTES = 4 * T
-WARM_PASSES = 4
 TAB0_AT = 12288
 TAB1_AT = TAB0_AT + TAB_BYTES + 6144
 STAGE_AT = TAB1_AT + TAB_BYTES
@@ -158,9 +157,6 @@ def tile_list_invoice_fraud_screen_kernel(tc, tab_words, tab_scales, offs, w1, w
             cols = slice(P * t, P * (t + 1))
             mm(diff[s, t][:], w1q[a][:, cols].bitcast(FP8X4), w1_sc[a][:, cols], moving(a, s), False, a == 1)
 
-        for i in range(WARM_PASSES):
-            mm(diff[1, PACK - 1][:], w2[:, 0, :2 * P].bitcast(FP4X4), rows[:, SC_W2:SC_W2 + P],
-               (w1q[0][:].bitcast(FP8X4), w1_sc[0][:]), True, True)
         for s in range(HALVES):
             pass_w2(0, s)
             for t in range(PACK):

@@ -79,9 +79,9 @@ def tile_list_invoice_fraud_screen_kernel(tc, tab_words, tab_scales, offs, w1, w
 
         tab = [placed([P, T], I32, "tab0", TAB0_AT), placed([P, T], I32, "tab1", TAB1_AT)]
         w2_raw = placed([P, PASSES, 2 * H], U8, "w2_raw", W2_RAW_AT)
-        nc.sync.dma_start(offsets[:], offs)
         w1_first = placed([P, PACK, H], F32, "w1_first", W1_AT)
         load_w1(w1_first, 0, slice(0, H))
+        nc.sync.dma_start(offsets[:], offs)
         load_rows(rows[0:P:4, SC_W5:], w5_scales)
         load_rows(w23_sc_raw[0:P:4, 0, :], w2_scales)
         load_rows(w23_sc_raw[0:P:4, 1, :], w3_scales)
@@ -248,8 +248,9 @@ def tile_list_invoice_fraud_screen_kernel(tc, tab_words, tab_scales, offs, w1, w
         round_h(1)
         quant_h(1)
         nc.sync.dma_start(out2_v, hq[:].bitcast(I32))
+        direct(0)
+        scores(0)
         for r in range(4):
-            nc.sync.dma_start(out_3[0, r:16:4, :].bitcast(I32), h_sc[r:P:32, :].bitcast(I32))
-        for s in range(HALVES):
-            direct(s)
-            scores(s)
+            nc.scalar.dma_start(out_3[0, r:16:4, :].bitcast(I32), h_sc[r:P:32, :].bitcast(I32))
+        direct(1)
+        scores(1)

@@ -25,6 +25,8 @@ HALVES = S // HALF
 NBLK = N // P
 BANKS = 8
 SC_W2, SC_W3, SC_W5, SC_COLS = S, S + H, S + 2 * H, S + 2 * H + N
+PLANE_PITCH = 2560
+SHIFT = 32
 TAB_BYTES = 4 * T
 TAB0_AT = 12288
 TAB1_AT = TAB0_AT + TAB_BYTES + 6144
@@ -43,10 +45,10 @@ def tile_list_invoice_fraud_screen_kernel(tc, tab_words, tab_scales, offs, w1, w
         psum = ctx.enter_context(tc.psum_pool(name="psum", bufs=1))
 
         def held(shape, dtype, name):
-            return keep.tile(shape, dtype, name=name, align_bytes=64)
+            return keep.tile(shape, dtype, name=name, align_bytes=256)
 
         def placed(shape, dtype, name, offset):
-            return reuse.tile(shape, dtype, name=name, align_bytes=64, offset=offset)
+            return reuse.tile(shape, dtype, name=name, align_bytes=256, offset=offset)
 
         taken = []
 
@@ -58,14 +60,14 @@ def tile_list_invoice_fraud_screen_kernel(tc, tab_words, tab_scales, offs, w1, w
         tab_sc = placed([P, T], U8, "tab_sc", STAGE_AT)
         w23_sc_raw = held([P, 2, H], U8, "w23_sc_raw")
         rows = held([P, SC_COLS], U8, "rows")
-        planes = held([P, PASSES, SC_COLS], U8, "planes")
+        planes = held([P, PASSES, PLANE_PITCH], U8, "planes")
         warm_in = held([P, 8], F32, "warm_in")
         warm_out = held([P, 8], F32, "warm_out")
 
         nc.vector.memset(w23_sc_raw[:].bitcast(I32), 0)
         nc.vector.memset(tab_sc[:].bitcast(I32), 0)
         nc.gpsimd.memset(warm_in[:], 0.0)
-        nc.gpsimd.memset(planes[:].bitcast(I32), 0)
+        nc.gpsimd.memset(planes[:, :, :SC_COLS].bitcast(I32), 0)
         nc.scalar.activation(warm_out[:], warm_in[:], ACT.Silu)
 
         def load_rows(dst, src):
@@ -95,14 +97,14 @@ def tile_list_invoice_fraud_screen_kernel(tc, tab_words, tab_scales, offs, w1, w
         nc.vector.tensor_copy(v_sc[:], tab_sc[:].indirect(offsets[:]))
         nc.vector.tensor_copy(rows[:, :S].bitcast(I32), v_sc[:].bitcast(I32))
         for q in (0, 2, 1, 3):
-            nc.sync.dma_start(planes[32 * q:32 * q + 4].bitcast(I32), rows[32 * q:32 * q + 32:4, :].bitcast(I32))
+            nc.sync.dma_start(planes[32 * q:32 * q + 4, :, :SC_COLS].bitcast(I32), rows[32 * q:32 * q + 32:4, :].bitcast(I32))
         load_table(1)
 
         v = {}
 
         def gather(a, s):
-            v[a, s] = held([P, HALF], U32, "v%d%d" % (a, s))
-            nc.vector.tensor_copy(v[a, s][:], tab[a][:].bitcast(U32).indirect(offsets[:, 32 * s:32 * (s + 1)]))
+            v[a, s] = held([P, SHIFT + HALF], U32, "v%d%d" % (a, s))
+            nc.vector.tensor_copy(v[a, s][:, SHIFT:], tab[a][:].bitcast(U32).indirect(offsets[:, 32 * s:32 * (s + 1)]))
 
         w1q = [held([P, H], U32, "w1q%d" % a) for a in range(PASSES)]
         w1_sc = [placed([P, H], U8, "w1_sc0", STAGE_AT + 2048), held([P, H], U8, "w1_sc1")]
@@ -139,7 +141,7 @@ def tile_list_invoice_fraud_screen_kernel(tc, tab_words, tab_scales, offs, w1, w
         nc.sync.dma_start(prior_sb[:], prior.rearrange("(b p) j -> p b j", p=P))
 
         def moving(a, s):
-            return v[a, s][:].bitcast(FP8X4), planes[:, a, HALF * s:HALF * (s + 1)]
+            return v[a, s][:, SHIFT:].bitcast(FP8X4), planes[:, a, HALF * s:HALF * (s + 1)]
 
         def plane(a, first, block):
             return planes[:, a, first + P * block:first + P * (block + 1)]
@@ -171,7 +173,7 @@ def tile_list_invoice_fraud_screen_kernel(tc, tab_words, tab_scales, offs, w1, w
 
         h = [held([P, PACK, HALF], F32, "h%d" % s) for s in range(HALVES)]
         hg = [held([P, HALF, PACK], BF16, "hg%d" % s) for s in range(HALVES)]
-        hq = held([P, S], U32, "hq")
+        hq = held([P, SHIFT + S], U32, "hq")[:, SHIFT:]
         h_sc = held([P, S], U8, "h_sc")
         out1_v = out_1.rearrange("(p t) j -> p t j", t=PACK)
         out2_v = out_2[0].rearrange("p m i -> p (m i)").bitcast(I32)
@@ -247,7 +249,7 @@ def tile_list_invoice_fraud_screen_kernel(tc, tab_words, tab_scales, offs, w1, w
             add_third(1, t)
         round_h(1)
         quant_h(1)
-        nc.sync.dma_start(out2_v, hq[:].bitcast(I32))
+        nc.sync.dma_start(out2_v, hq.bitcast(I32))
         direct(0)
         scores(0)
         for r in range(4):

from contextlib import ExitStack

import concourse.mybir as mybir

K, H, N, T, S = 1024, 512, 384, 4096, 1024
FLOPS = 2 * S * (3 * K * H + H * N + K * N)

F32 = mybir.dt.float32
BF16 = mybir.dt.bfloat16
I32 = mybir.dt.int32
U32 = mybir.dt.uint32
U16 = mybir.dt.uint16
U8 = mybir.dt.uint8
FP8X4 = mybir.dt.float8_e4m3fn_x4
FP4X4 = mybir.dt.float4_e2m1fn_x4
ACT = mybir.ActivationFunctionType
ALU = mybir.AluOpType

P = 128
PACK = 4
K_PASS = P * PACK
PASSES = K // K_PASS
HALF = 512
HALVES = S // HALF
NBLK = N // P
BANKS = 8
SC_W2, SC_W3, SC_W5, SC_COLS = S, S + H, S + 2 * H, S + 2 * H + N
PLANE_PITCH = 2560
SHIFT = 32
TAB_BYTES = 4 * T
TAB0_AT = 12288
TAB1_AT = TAB0_AT + TAB_BYTES + 6144
STAGE_AT = TAB1_AT + TAB_BYTES
W1_AT = STAGE_AT + 4096 + 512
W2_RAW_AT = W1_AT + 8192 + 4096


def tile_list_invoice_fraud_screen_kernel(tc, tab_words, tab_scales, offs, w1, w2_words, w2_scales,
                                                   w3_words, w3_scales, w4, w5_words, w5_scales, prior,
                                                   out_0, out_1, out_2, out_3):
    nc = tc.nc
    with ExitStack() as ctx:
        keep = ctx.enter_context(tc.tile_pool(name="keep", bufs=1))
        reuse = ctx.enter_context(tc.tile_pool(name="reuse", bufs=1))
        psum = ctx.enter_context(tc.psum_pool(name="psum", bufs=1))

        def held(shape, dtype, name):
            return keep.tile(shape, dtype, name=name, align_bytes=256)

        def placed(shape, dtype, name, offset):
            return reuse.tile(shape, dtype, name=name, align_bytes=256, offset=offset)

        taken = []

        def bank():
            taken.append(len(taken) % BANKS)
            return psum.tile([P, HALF], F32, name="bank%d" % taken[-1])

        offsets = keep.tile([P, S // 16], U16, name="offsets")
        tab_sc = placed([P, T], U8, "tab_sc", STAGE_AT)
        w23_sc_raw = held([P, 2, H], U8, "w23_sc_raw")
        rows = held([P, SC_COLS], U8, "rows")
        planes = held([P, PASSES, PLANE_PITCH], U8, "planes")
        warm_in = held([P, 8], F32, "warm_in")
        warm_out = held([P, 8], F32, "warm_out")

        nc.vector.memset(w23_sc_raw[:].bitcast(I32), 0)
        nc.vector.memset(tab_sc[:].bitcast(I32), 0)
        nc.gpsimd.memset(warm_in[:], 0.0)
        nc.gpsimd.memset(planes[:, :, :SC_COLS].bitcast(I32), 0)
        nc.scalar.activation(warm_out[:], warm_in[:], ACT.Silu)

        def load_rows(dst, src):
            nc.sync.dma_start(dst.bitcast(I32), src.rearrange("a q n -> q a n").bitcast(I32))

        def load_table(a):
            nc.sync.dma_start(tab[a][:], tab_words[a].rearrange("p t i -> p (t i)").bitcast(I32))

        def load_w1(dst, a, cols):
            nc.sync.dma_start(dst[:], w1[K_PASS * a:K_PASS * (a + 1), cols].rearrange("(p j) c -> p j c", j=PACK))

        tab = [placed([P, T], I32, "tab0", TAB0_AT), placed([P, T], I32, "tab1", TAB1_AT)]
        w2_raw = placed([P, PASSES, 2 * H], U8, "w2_raw", W2_RAW_AT)
        w1_first = placed([P, PACK, H], F32, "w1_first", W1_AT)
        load_w1(w1_first, 0, slice(0, H))
        nc.sync.dma_start(offsets[:], offs)
        load_rows(rows[0:P:4, SC_W5:], w5_scales)
        load_rows(w23_sc_raw[0:P:4, 0, :], w2_scales)
        load_rows(w23_sc_raw[0:P:4, 1, :], w3_scales)
        load_rows(tab_sc[0:P:4, :], tab_scales)
        nc.sync.dma_start(w2_raw[:].bitcast(I32), w2_words.rearrange("a p c -> p a c").bitcast(I32))
        load_table(0)

        v_sc = placed([P, S], U8, "v_sc", TAB1_AT)
        nc.vector.tensor_copy(rows[:, SC_W2:SC_W5].rearrange("p (w t c i) -> p w c t i", w=2, t=PACK, i=16),
                              w23_sc_raw[:].rearrange("p w (c i t) -> p w c t i", t=PACK, i=16))
        nc.vector.tensor_copy(v_sc[:], tab_sc[:].indirect(offsets[:]))
        nc.vector.tensor_copy(rows[:, :S].bitcast(I32), v_sc[:].bitcast(I32))
        for q in (0, 2, 1, 3):
            nc.sync.dma_start(planes[32 * q:32 * q + 4, :, :SC_COLS].bitcast(I32), rows[32 * q:32 * q + 32:4, :].bitcast(I32))
        load_table(1)

        v = {}

        def gather(a, s):
            v[a, s] = held([P, SHIFT + HALF], U32, "v%d%d" % (a, s))
            nc.vector.tensor_copy(v[a, s][:, SHIFT:], tab[a][:].bitcast(U32).indirect(offsets[:, 32 * s:32 * (s + 1)]))

        w1q = [held([P, H], U32, "w1q%d" % a) for a in range(PASSES)]
        w1_sc = [placed([P, H], U8, "w1_sc0", STAGE_AT + 2048), held([P, H], U8, "w1_sc1")]
        w1g = {(a, u): held([P, PACK, P // 2, PACK], BF16, "w1g%d%d" % (a, u)) for a, u in ((0, 0), (1, 0), (1, 1))}
        w1g[0, 1] = placed([P, PACK, P // 2, PACK], BF16, "w1g01", STAGE_AT)

        def prepare_w1(a, halves):
            dst = [w1g[a, u][:].rearrange("p t m j -> p m t j") for u in range(2)]
            src = [half.rearrange("p j (m t) -> p m t j", t=PACK) for half in halves]
            nc.scalar.activation(dst[0], src[0], ACT.Copy, scale=-1.0)
            nc.vector.tensor_scalar(dst[1], src[1], -1.0, None, ALU.mult)
            for t in range(PACK):
                for u in range(2):
                    cols = slice(P * t + P // 2 * u, P * t + P // 2 * (u + 1))
                    nc.vector.quantize_mx(out=w1q[a][:, cols].bitcast(FP8X4), scales=w1_sc[a][:, cols],
                                          in_=w1g[a, u][:, t].rearrange("p m j -> p (m j)"))

        prepare_w1(0, [w1_first[:, :, :H // 2], w1_first[:, :, H // 2:]])
        w2 = placed([P, PASSES, 2 * H], U8, "w2", STAGE_AT + 2048 + 512)
        nc.vector.tensor_copy(w2[:].bitcast(U16).rearrange("p a (t c i) -> p a c t i", t=PACK, i=8),
                              w2_raw[:].bitcast(U16).rearrange("p a (c i t) -> p a c t i", t=PACK, i=8))
        gather(0, 0)
        gather(0, 1)
        w1_last = [placed([P, PACK, H // 2], F32, "w1_last%d" % u, W1_AT + 4096 * u) for u in range(2)]
        for u in range(2):
            load_w1(w1_last[u], 1, slice(H // 2 * u, H // 2 * (u + 1)))
        w3_raw = placed([P, PASSES, H], I32, "w3_raw", W2_RAW_AT + 1024 - 4096)
        nc.sync.dma_start(w3_raw[:], w3_words.rearrange("a p c i -> p a (c i)").bitcast(I32))
        w4_raw = placed([P, PACK, N], F32, "w4_raw", W2_RAW_AT + 1024)
        w5 = placed([P, PASSES, 2 * N], U8, "w5", TAB0_AT + 1024 + 12288)
        prior_sb = placed([P, NBLK, S], F32, "prior_sb", TAB0_AT + 1024 - 4 * NBLK * S)
        nc.sync.dma_start(w4_raw[:], w4.rearrange("(p j) n -> p j n", j=PACK))
        nc.sync.dma_start(w5[:].bitcast(I32), w5_words.rearrange("a p c -> p a c").bitcast(I32))
        nc.sync.dma_start(prior_sb[:], prior.rearrange("(b p) j -> p b j", p=P))

        def moving(a, s):
            return v[a, s][:, SHIFT:].bitcast(FP8X4), planes[:, a, HALF * s:HALF * (s + 1)]

        def plane(a, first, block):
            return planes[:, a, first + P * block:first + P * (block + 1)]

        def mm(acc, lhsT, lhsT_scale, rhs, start, stop):
            nc.tensor.matmul_mx(out=acc, lhsT=lhsT, lhsT_scale=lhsT_scale, rhs=rhs[0], rhs_scale=rhs[1], start=start, stop=stop)

        diff = {(s, t): bank() for s in range(HALVES) for t in range(PACK)}

        def pass_w2(a, s):
            for t in range(PACK):
                mm(diff[s, t][:], w2[:, a, 2 * P * t:2 * P * (t + 1)].bitcast(FP4X4), plane(a, SC_W2, t), moving(a, s), a == 0, False)

        def pass_w1(a, s, t):
            cols = slice(P * t, P * (t + 1))
            mm(diff[s, t][:], w1q[a][:, cols].bitcast(FP8X4), w1_sc[a][:, cols], moving(a, s), False, a == 1)

        for s in range(HALVES):
            pass_w2(0, s)
            for t in range(PACK):
                pass_w1(0, s, t)
        gather(1, 0)
        pass_w2(1, 0)
        gather(1, 1)
        prepare_w1(1, [w1_last[0][:], w1_last[1][:]])
        w3 = held([P, PASSES, H], I32, "w3")
        nc.vector.tensor_copy(w3[:].rearrange("p a (t c i) -> p a c t i", t=PACK, i=4),
                              w3_raw[:].rearrange("p a (c i t) -> p a c t i", t=PACK, i=4))

        h = [held([P, PACK, HALF], F32, "h%d" % s) for s in range(HALVES)]
        hg = [held([P, HALF, PACK], BF16, "hg%d" % s) for s in range(HALVES)]
        hq = held([P, SHIFT + S], U32, "hq")[:, SHIFT:]
        h_sc = held([P, S], U8, "h_sc")
        out1_v = out_1.rearrange("(p t) j -> p t j", t=PACK)
        out2_v = out_2[0].rearrange("p m i -> p (m i)").bitcast(I32)
        mag = {}

        def close_diff(s):
            for t in range(PACK):
                pass_w1(1, s, t)
                mag[s, t] = held([P, HALF], F32, "mag%d%d" % (s, t))
                nc.scalar.activation(mag[s, t][:], diff[s, t][:], ACT.Abs)

        def add_third(s, t):
            acc = bank()
            for a in range(PASSES):
                mm(acc[:], w3[:, a, P * t:P * (t + 1)].bitcast(FP8X4), plane(a, SC_W3, t), moving(a, s), a == 0, a == 1)
            nc.vector.tensor_tensor(h[s][:, t, :], mag[s, t][:], acc[:], ALU.add)
            if t == PACK - 1:
                nc.sync.dma_start(out1_v[:, :, HALF * s:HALF * (s + 1)], h[s][:])

        def round_h(s):
            dst = hg[s][:].rearrange("p (c i) t -> p c t i", i=4)
            src = h[s][:].rearrange("p t (c i) -> p c t i", i=4)
            for c0, c1 in ((0, 40), (40, 80)):
                nc.scalar.copy(dst[:, c0:c1], src[:, c0:c1])
            nc.gpsimd.tensor_scalar(hg[s][:, 320:, :], h[s][:, :, 320:].rearrange("p t j -> p j t"), 1.0, 0.0, ALU.mult, ALU.add)

        def quant_h(s):
            cols = slice(HALF * s, HALF * (s + 1))
            nc.vector.quantize_mx(out=hq[:, cols].bitcast(FP8X4), scales=h_sc[:, cols], in_=hg[s][:].rearrange("p c t -> p (c t)"))

        w4g = held([P, N, PACK], BF16, "w4g")
        w4q = held([P, N], U32, "w4q")
        w4_sc = held([P, N], U8, "w4_sc")

        def quant_w4():
            nc.gpsimd.tensor_scalar(w4g[:], w4_raw[:].rearrange("p j n -> p n j"), 1.0, 0.0, ALU.mult, ALU.add)
            flat = w4g[:].rearrange("p n j -> p (n j)")
            for n0, n1 in ((0, 256), (256, N)):
                nc.vector.quantize_mx(out=w4q[:, n0:n1].bitcast(FP8X4), scales=w4_sc[:, n0:n1], in_=flat[:, 4 * n0:4 * n1])

        base = {}

        def direct(s):
            for b in range(NBLK):
                acc = bank()
                for a in range(PASSES):
                    mm(acc[:], w5[:, a, 2 * P * b:2 * P * (b + 1)].bitcast(FP4X4), plane(a, SC_W5, b), moving(a, s), a == 0, a == 1)
                base[s, b] = held([P, HALF], F32, "base%d%d" % (s, b))
                nc.vector.tensor_tensor(base[s, b][:], prior_sb[:, b, HALF * s:HALF * (s + 1)], acc[:], ALU.add)

        def scores(s):
            cols = slice(HALF * s, HALF * (s + 1))
            for b in range(NBLK):
                acc = bank()
                mm(acc[:], w4q[:, P * b:P * (b + 1)].bitcast(FP8X4), w4_sc[:, P * b:P * (b + 1)],
                   (hq[:, cols].bitcast(FP8X4), h_sc[:, cols]), True, True)
                gate = held([P, HALF], F32, "gate%d%d" % (s, b))
                nc.scalar.activation(gate[:], acc[:], ACT.Silu)
                y = held([P, HALF], F32, "y%d%d" % (s, b))
                adder = nc.gpsimd if s == 0 and b != 1 else nc.vector
                adder.tensor_tensor(y[:], gate[:], base[s, b][:], ALU.add)
                nc.sync.dma_start(out_0[P * b:P * (b + 1), cols], y[:])

        close_diff(0)
        for t in range(PACK):
            add_third(0, t)
        pass_w2(1, 1)
        close_diff(1)
        quant_w4()
        round_h(0)
        quant_h(0)
        for t in range(PACK):
            add_third(1, t)
        round_h(1)
        quant_h(1)
        nc.sync.dma_start(out2_v, hq.bitcast(I32))
        direct(0)
        scores(0)
        for r in range(4):
            nc.scalar.dma_start(out_3[0, r:16:4, :].bitcast(I32), h_sc[r:P:32, :].bitcast(I32))
        direct(1)
        scores(1)
